import numpy as np
import ml_dtypes


def mxq(x, axis, fmt="e4m3"):
    dtype, down = {"e4m3": (ml_dtypes.float8_e4m3fn, 7), "e5m2": (ml_dtypes.float8_e5m2, 14)}[fmt]
    v = np.moveaxis(np.asarray(x, np.float32).astype(ml_dtypes.bfloat16).astype(np.float64), axis, -1)
    blocks = v.reshape(v.shape[:-1] + (-1, 32))
    amax = np.abs(blocks).max(-1, keepdims=True)
    byte = np.maximum(np.where(amax > 0, np.frexp(amax)[1] - 1 + 127, 0) - down, 1)
    scale = np.exp2(byte - 127.0)
    codes = (blocks / scale).astype(np.float32).astype(dtype).astype(np.float64)
    return np.moveaxis((codes * scale).reshape(v.shape), -1, axis)


WIDE = False


def mx_kscale(k):
    if not WIDE:
        return np.ones(k)
    levels = np.array([10, -10, 5, -5, 0])
    if k % 512:
        return np.exp2(np.random.permutation(np.resize(levels, k // 32))).repeat(32)
    a = np.empty((k // 512, 16))
    for p in range(k // 512):
        a[p, :8] = np.random.permutation(np.resize(levels, 8))
        for g in range(8):
            far = levels[np.abs(levels - a[p, g]) >= 10]
            a[p, g + 8] = far[np.random.randint(len(far))]
    return np.exp2(a.ravel()).repeat(32)


def f64(x):
    return np.asarray(x).astype(np.float64)


def striped(idx):
    return np.tile(np.asarray(idx).reshape(-1, 16).T, (8, 1)).astype(np.uint16)


def unstriped(offs):
    return offs[:16].T.reshape(-1).astype(np.int64)


E2M1 = np.array([0.0, 0.5, 1.0, 1.5, 2.0, 3.0, 4.0, 6.0, -0.0, -0.5, -1.0, -1.5, -2.0, -3.0, -4.0, -6.0])


def pack_weight(w, fmt):
    k, n = w.shape
    w = f64(np.asarray(w, np.float32).astype(ml_dtypes.bfloat16)).reshape(k // 32, 32, n)
    amax = np.abs(w).max(1)
    if fmt == "e4m3":
        byte = np.frexp(amax)[1] - 1 + 127 - 7
    else:
        mant, ex = np.frexp(amax / 6.0)
        byte = np.where(mant > 0.5, ex, ex - 1) + 127
    byte = np.clip(np.where(amax > 0, byte, 1), 1, 254)
    scaled = (w * np.exp2(127.0 - byte)[:, None, :]).reshape(k, n).astype(np.float32)
    by_word = np.ascontiguousarray(scaled.reshape(k // 512, 128, 4, n).transpose(0, 1, 3, 2))
    if fmt == "e4m3":
        words = by_word.astype(ml_dtypes.float8_e4m3fn).view(np.uint8)
    else:
        c = by_word.astype(ml_dtypes.float4_e2m1fn).view(np.uint8) & 0xF
        words = (c[..., 0::2] | (c[..., 1::2] << 4)).reshape(k // 512, 128, 2 * n)
    return np.ascontiguousarray(words), np.ascontiguousarray(byte.astype(np.uint8).reshape(k // 512, 16, n))


def unpack_weight(words, scales, fmt):
    g, _, n = scales.shape
    words = np.ascontiguousarray(words).reshape(g, 128, n, -1)
    if fmt == "e4m3":
        vals = words.view(ml_dtypes.float8_e4m3fn).astype(np.float64)
    else:
        nib = np.empty((g, 128, n, 4), np.uint8)
        nib[..., 0::2] = words & 0xF
        nib[..., 1::2] = words >> 4
        vals = E2M1[nib]
    vals = vals * np.repeat(np.exp2(scales.astype(np.float64) - 127.0), 8, axis=1)[..., None]
    return vals.transpose(0, 1, 3, 2).reshape(g * 512, n)


def bf(x):
    return np.asarray(x, np.float32).astype(ml_dtypes.bfloat16)


def planes(Y):
    r, m = Y.shape
    b = f64(bf(Y)).reshape(r // 32, 32, m)
    amax = np.abs(b).max(1)
    byte = np.clip(np.where(amax > 0, np.frexp(amax)[1] - 1 + 127 - 7, 1), 1, 254)
    codes = (b * np.exp2(127.0 - byte)[:, None, :]).reshape(r, m).astype(np.float32).astype(ml_dtypes.float8_e4m3fn).view(np.uint8)
    words = codes.reshape(r // 512, 128, 4, m).transpose(0, 1, 3, 2)
    return np.ascontiguousarray(words), np.ascontiguousarray(byte.astype(np.uint8).reshape(r // 512, 16, m))


D, T, I, Q, E = 512, 1024, 512, 256, 512


def setup_inputs():
    n = np.random.standard_normal
    idx = np.random.permutation(T)[:I]
    fd = mx_kscale(D)
    fi = mx_kscale(I)
    keysp = pack_weight(n((D, T)) / fd[:, None], "e2m1")
    return {
        "query": (n((D, Q)) * 0.25 / np.sqrt(D) * fd[:, None]).astype(np.float32),
        "keys_words": keysp[0],
        "keys_scales": keysp[1],
        "size": (np.random.uniform(0.5, 2.0, (1, I)) * fi).astype(np.float32),
        "vals": (n((E, T))).astype(np.float32),
        "first": (n((E, T))).astype(np.float32),
        "lam": (np.random.uniform(0.3, 0.8, (1, I))).astype(np.float32),
        "vsc": (np.random.uniform(0.5, 2.0, (I, 1)) / fi[:, None]).astype(np.float32),
        "offs": striped(idx),
    }


def reference(query, keys_words, keys_scales, size, vals, first, lam, vsc, offs):
    idx = unstriped(offs)
    keysu = unpack_weight(keys_words, keys_scales, "e2m1")
    queryq = mxq(f64(query), 0, "e4m3")
    keysidxg = keysu[:, idx]
    a = queryq.T @ keysidxg
    p = np.exp(a - np.max(a, axis=1, keepdims=True))
    w = p * f64(size) / np.sum(p, axis=1, keepdims=True)
    wt = w.T
    vm = f64(vals)[:, idx] * f64(lam) + f64(first)[:, idx] * (1.0 - f64(lam))
    vt = vm.T
    vv = vt * f64(vsc)
    vvq = mxq(vv, 0, "e4m3")
    wtq = mxq(wt, 0, "e4m3")
    o = vvq.T @ wtq
    words, scales = planes(o)
    return o, words, scales

@@ -1,0 +1,230 @@
+from contextlib import ExitStack
+
+import concourse.mybir as mybir
+from concourse.masks import make_identity
+
+D, T, I, Q, E = 512, 1024, 512, 256, 512
+FLOPS = 2 * Q * I * D + 2 * E * I * Q
+
+F32 = mybir.dt.float32
+BF16 = mybir.dt.bfloat16
+I32 = mybir.dt.int32
+U32 = mybir.dt.uint32
+U16 = mybir.dt.uint16
+U8 = mybir.dt.uint8
+FP8X4 = mybir.dt.float8_e4m3fn_x4
+FP4X4 = mybir.dt.float4_e2m1fn_x4
+ALU = mybir.AluOpType
+ACT = mybir.ActivationFunctionType
+AXIS_X = mybir.AxisListType.X
+
+P = 128
+PACK = 4
+Q_BLOCKS = Q // P
+
+
+def tile_attend_valueresidual_pl_kernel(
+    tc, query, keys_words, keys_scales, size, vals, first, lam, vsc, offs, out_0, out_1, out_2
+):
+    nc = tc.nc
+    with ExitStack() as ctx:
+        keep = ctx.enter_context(tc.tile_pool(name="keep", bufs=1))
+        psum = ctx.enter_context(tc.psum_pool(name="psum", bufs=1))
+        psum2 = ctx.enter_context(tc.psum_pool(name="psum2", bufs=2))
+
+        offsets = keep.tile([P, I // 16], U16, name="offsets")
+        nc.sync.dma_start(offsets[:], offs)
+
+        key_scales = keep.tile([P, T], U8, name="key_scales", align_bytes=64)
+        nc.gpsimd.memset(key_scales[:].bitcast(I32), 0)
+
+        lam_col = keep.tile([P, PACK], F32, name="lam_col")
+        nc.gpsimd.dma_start(lam_col[:], lam.rearrange("o (p t) -> (o p) t", t=PACK))
+        vsc_col = keep.tile([P, PACK], F32, name="vsc_col")
+        nc.gpsimd.dma_start(vsc_col[:], vsc.rearrange("(p t) o -> p (t o)", t=PACK))
+        key_words = keep.tile([P, T], U16, name="key_words", align_bytes=64)
+        nc.sync.dma_start(key_words[:].bitcast(I32), keys_words[0].bitcast(I32))
+        for quad in range(4):
+            nc.sync.dma_start(
+                key_scales[32 * quad : 32 * quad + 4, :].bitcast(I32),
+                keys_scales[0, 4 * quad : 4 * quad + 4, :].bitcast(I32),
+            )
+
+        vals_planes = vals.rearrange("(p j) n -> p j n", j=PACK)
+        first_planes = first.rearrange("(p j) n -> p j n", j=PACK)
+        vals_sb = [keep.tile([P, T], F32, name=f"vals_sb{j}") for j in range(PACK)]
+        first_sb = [keep.tile([P, T], F32, name=f"first_sb{j}") for j in range(PACK)]
+        query_sb = keep.tile([P, PACK, Q], F32, name="query_sb")
+        nc.sync.dma_start(query_sb[:], query.rearrange("(p j) q -> p j q", j=PACK))
+        nc.sync.dma_start(vals_sb[0][:], vals_planes[:, 0, :])
+        nc.sync.dma_start(first_sb[0][:], first_planes[:, 0, :])
+        for j in range(1, PACK):
+            nc.sync.dma_start(vals_sb[j][:], vals_planes[:, j, :])
+            nc.sync.dma_start(first_sb[j][:], first_planes[:, j, :])
+
+        ident = keep.tile([P, P], F32, name="ident")
+        make_identity(nc, ident[:])
+        size_col = keep.tile([P, PACK], F32, name="size_col")
+        nc.gpsimd.dma_start(size_col[:], size.rearrange("o (p t) -> (o p) t", t=PACK))
+
+        vals_factor = keep.tile([P, PACK], F32, name="vals_factor")
+        nc.vector.tensor_tensor(vals_factor[:], lam_col[:], vsc_col[:], ALU.mult)
+        neg_first_factor = keep.tile([P, PACK], F32, name="neg_first_factor")
+        nc.vector.scalar_tensor_tensor(
+            neg_first_factor[:], lam_col[:], 1.0, vsc_col[:], ALU.subtract, ALU.mult
+        )
+        factor_rows = []
+        for name, col, sign in (("vals", vals_factor, 1.0), ("first", neg_first_factor, -1.0)):
+            spread = psum2.tile([P, PACK, P], F32, name="turn_ps", tag="turn_ps")
+            for t in range(PACK):
+                nc.tensor.transpose(spread[:, t, :], col[:, t : t + 1].to_broadcast([P, P]), ident[:])
+            row = keep.tile([P, I], F32, name=f"{name}_row")
+            nc.scalar.activation(
+                row[:].rearrange("m (p t) -> m p t", t=PACK),
+                spread[:].rearrange("m t p -> m p t"),
+                ACT.Copy,
+                scale=sign,
+            )
+            factor_rows.append(row)
+        vals_row, first_row = factor_rows
+
+        key_words_g = keep.tile([P, I], U16, name="key_words_g", align_bytes=64)
+        nc.vector.tensor_copy(key_words_g[:], key_words[:].indirect(offsets[:]))
+        key_scales_g = keep.tile([P, I], U8, name="key_scales_g", align_bytes=64)
+        nc.vector.tensor_copy(key_scales_g[:], key_scales[:].indirect(offsets[:]))
+
+        query_bf = keep.tile([P, Q, PACK], BF16, name="query_bf", tag="query_stage", align_bytes=64)
+        nc.scalar.copy(
+            query_bf[:].rearrange("p (c i) t -> p c t i", i=4),
+            query_sb[:].rearrange("p t (c i) -> p c t i", i=4),
+        )
+        query_codes = keep.tile([P, Q], U32, name="query_codes", align_bytes=64)
+        query_scales = keep.tile([P, Q], U8, name="query_scales", align_bytes=64)
+        nc.vector.quantize_mx(
+            out=query_codes[:].bitcast(FP8X4),
+            scales=query_scales[:],
+            in_=query_bf[:].rearrange("p q t -> p (q t)"),
+        )
+
+        normed = []
+        for b in range(Q_BLOCKS):
+            cols = slice(b * P, (b + 1) * P)
+            scores = psum.tile([P, I], F32, name=f"scores{b}")
+            nc.tensor.matmul_mx(
+                out=scores[:],
+                lhsT=query_codes[:, cols].bitcast(FP8X4),
+                lhsT_scale=query_scales[:, cols],
+                rhs=key_words_g[:].bitcast(FP4X4),
+                rhs_scale=key_scales_g[:],
+                start=True,
+                stop=True,
+            )
+            neg_max = keep.tile([P, 1], F32, name=f"neg_max{b}")
+            nc.vector.tensor_reduce(neg_max[:], scores[:], AXIS_X, ALU.max, negate=True)
+            probs = keep.tile([P, PACK, P], F32, name=f"probs{b}")
+            row_sum = keep.tile([P, 1], F32, name=f"row_sum{b}")
+            nc.scalar.activation(
+                probs[:],
+                scores[:].rearrange("q (s t) -> q t s", t=PACK),
+                ACT.Exp,
+                bias=neg_max[:],
+                accum_out=row_sum[:],
+            )
+            inv_sum = keep.tile([P, 1], F32, name=f"inv_sum{b}")
+            nc.vector.reciprocal(inv_sum[:], row_sum[:])
+            norm = keep.tile([P, PACK, P], F32, name=f"norm{b}")
+            nc.scalar.activation(norm[:], probs[:], ACT.Copy, scale=inv_sum[:])
+            normed.append(norm)
+
+        weights_planar = keep.tile([P, PACK, Q], BF16, name="weights_planar", tag="stage", align_bytes=64)
+        for half in range(2):
+            turned = psum2.tile([P, 2, Q], F32, name="turn_ps", tag="turn_ps")
+            for u in range(2):
+                for b in range(Q_BLOCKS):
+                    nc.tensor.transpose(
+                        turned[:, u, b * P : (b + 1) * P], normed[b][:, 2 * half + u, :], ident[:]
+                    )
+            for u in range(2):
+                t = 2 * half + u
+                nc.scalar.activation(
+                    weights_planar[:, t, :], turned[:, u, :], ACT.Copy, scale=size_col[:, t : t + 1]
+                )
+        weights_bf = keep.tile([P, Q, PACK], BF16, name="weights_bf", align_bytes=64)
+        nc.scalar.copy(
+            weights_bf[:].rearrange("p (c i) t -> p c t i", i=4),
+            weights_planar[:].rearrange("p t (c i) -> p c t i", i=4),
+        )
+        weight_codes = keep.tile([P, Q], U32, name="weight_codes", align_bytes=64)
+        weight_scales = keep.tile([P, Q], U8, name="weight_scales", align_bytes=64)
+        nc.vector.quantize_mx(
+            out=weight_codes[:].bitcast(FP8X4),
+            scales=weight_scales[:],
+            in_=weights_bf[:].rearrange("p q t -> p (q t)"),
+        )
+
+        result_ps = [psum.tile([P, PACK, P], F32, name=f"result_ps{b}") for b in range(Q_BLOCKS)]
+        out_planes = out_0.rearrange("(p j) q -> p j q", j=PACK)
+        for j in range(PACK):
+            mixed = psum2.tile([P, PACK, P], F32, name="mixed_ps", tag="mixed_ps" if j < 2 else "turn_ps")
+            for step, (pool_sb, row) in enumerate(((vals_sb[j], vals_row), (first_sb[j], first_row))):
+                picked_tag = {(0, 0): "query_stage", (PACK - 1, 1): "stage"}.get((j, step), f"picked{j}_{step}")
+                picked = keep.tile([P, I], F32, name=f"picked{j}_{step}", tag=picked_tag, align_bytes=64)
+                nc.vector.tensor_tensor(picked[:], pool_sb[:].indirect(offsets[:]), row[:], ALU.mult)
+                by_place = picked[:].rearrange("e (s t) -> e t s", t=PACK)
+                for t in range(PACK):
+                    nc.tensor.matmul(
+                        mixed[:, t, :],
+                        by_place[:, t, :],
+                        ident[:],
+                        start=(step == 0 and t == 0),
+                        stop=(step == 1 and t == PACK - 1),
+                        is_transpose=True,
+                    )
+            value_bf = keep.tile(
+                [P, P, PACK], BF16, name=f"value_bf{j}", tag="stage" if j == 1 else f"value_bf{j}", align_bytes=64
+            )
+            nc.scalar.copy(value_bf[:], mixed[:].rearrange("s t m -> s m t"))
+            value_codes = keep.tile([P, P], U32, name=f"value_codes{j}", align_bytes=64)
+            value_scales = keep.tile([P, P], U8, name=f"value_scales{j}", align_bytes=64)
+            nc.vector.quantize_mx(
+                out=value_codes[:].bitcast(FP8X4),
+                scales=value_scales[:],
+                in_=value_bf[:].rearrange("s m t -> s (m t)"),
+            )
+            result = keep.tile([P, Q], F32, name=f"result{j}")
+            for b in range(Q_BLOCKS):
+                cols = slice(b * P, (b + 1) * P)
+                nc.tensor.matmul_mx(
+                    out=result_ps[b][:, j, :],
+                    lhsT=value_codes[:].bitcast(FP8X4),
+                    lhsT_scale=value_scales[:],
+                    rhs=weight_codes[:, cols].bitcast(FP8X4),
+                    rhs_scale=weight_scales[:, cols],
+                    start=True,
+                    stop=True,
+                )
+            if j == PACK - 1:
+                result_bf = keep.tile([P, Q, PACK], BF16, name="result_bf", align_bytes=64)
+                nc.vector.tensor_copy(result_bf[:, 0:P, :], result_ps[0][:].rearrange("p j q -> p q j"))
+                nc.scalar.copy(result_bf[:, P:Q, :], result_ps[1][:].rearrange("p j q -> p q j"))
+            for b in reversed(range(Q_BLOCKS)):
+                cols = slice(b * P, (b + 1) * P)
+                nc.scalar.copy(result[:, cols], result_ps[b][:, j, :])
+            nc.sync.dma_start(out_planes[:, j, :], result[:])
+
+        result_codes = keep.tile([P, Q], U32, name="result_codes", align_bytes=64)
+        result_scales = keep.tile([P, Q], U8, name="result_scales", align_bytes=64)
+        nc.vector.quantize_mx(
+            out=result_codes[:].bitcast(FP8X4),
+            scales=result_scales[:],
+            in_=result_bf[:].rearrange("p q j -> p (q j)"),
+        )
+        nc.sync.dma_start(
+            out_1[0].rearrange("p q j -> p (q j)").bitcast(I32), result_codes[:].bitcast(I32)
+        )
+        for quad in range(4):
+            queue = nc.scalar if quad % 2 == 0 else nc.sync
+            queue.dma_start(
+                out_2[0, 4 * quad : 4 * quad + 4, :].bitcast(I32),
+                result_scales[32 * quad : 32 * quad + 4, :].bitcast(I32),
+            )

@@ -35,46 +35,45 @@ def tile_attend_valueresidual_pl_kernel(
         offsets = keep.tile([P, I // 16], U16, name="offsets")
         nc.sync.dma_start(offsets[:], offs)
 
-        key_scales = keep.tile([P, T], U8, name="key_scales", align_bytes=64)
+        key_scales = keep.tile([P, T], U8, name="key_scales", tag="key_scales", align_bytes=64)
         nc.gpsimd.memset(key_scales[:].bitcast(I32), 0)
 
         lam_col = keep.tile([P, PACK], F32, name="lam_col")
-        nc.gpsimd.dma_start(lam_col[:], lam.rearrange("o (p t) -> (o p) t", t=PACK))
+        nc.sync.dma_start(lam_col[:], lam.rearrange("o (p t) -> (o p) t", t=PACK))
         vsc_col = keep.tile([P, PACK], F32, name="vsc_col")
-        nc.gpsimd.dma_start(vsc_col[:], vsc.rearrange("(p t) o -> p (t o)", t=PACK))
+        nc.sync.dma_start(vsc_col[:], vsc.rearrange("(p t) o -> p (t o)", t=PACK))
         key_words = keep.tile([P, T], U16, name="key_words", align_bytes=64)
         nc.sync.dma_start(key_words[:].bitcast(I32), keys_words[0].bitcast(I32))
+        vals_planes = vals.rearrange("(p j) n -> p j n", j=PACK)
+        first_planes = first.rearrange("(p j) n -> p j n", j=PACK)
+        vals_sb = [keep.tile([P, T], F32, name=f"vals_sb{j}", tag=f"vals_sb{j}", align_bytes=64) for j in range(PACK)]
+        first_sb = [keep.tile([P, T], F32, name=f"first_sb{j}", tag=f"first_sb{j}", align_bytes=64) for j in range(PACK)]
+        nc.sync.dma_start(vals_sb[0][:], vals_planes[:, 0, :])
+        query_sb = keep.tile([P, PACK, Q], F32, name="query_sb")
+        nc.sync.dma_start(query_sb[:], query.rearrange("(p j) q -> p j q", j=PACK))
         for quad in range(4):
             nc.sync.dma_start(
                 key_scales[32 * quad : 32 * quad + 4, :].bitcast(I32),
                 keys_scales[0, 4 * quad : 4 * quad + 4, :].bitcast(I32),
             )
-
-        vals_planes = vals.rearrange("(p j) n -> p j n", j=PACK)
-        first_planes = first.rearrange("(p j) n -> p j n", j=PACK)
-        vals_sb = [keep.tile([P, T], F32, name=f"vals_sb{j}") for j in range(PACK)]
-        first_sb = [keep.tile([P, T], F32, name=f"first_sb{j}") for j in range(PACK)]
-        query_sb = keep.tile([P, PACK, Q], F32, name="query_sb")
-        nc.sync.dma_start(query_sb[:], query.rearrange("(p j) q -> p j q", j=PACK))
-        nc.sync.dma_start(vals_sb[0][:], vals_planes[:, 0, :])
         nc.sync.dma_start(first_sb[0][:], first_planes[:, 0, :])
+        size_col = keep.tile([P, PACK], F32, name="size_col")
+        nc.sync.dma_start(size_col[:], size.rearrange("o (p t) -> (o p) t", t=PACK))
         for j in range(1, PACK):
             nc.sync.dma_start(vals_sb[j][:], vals_planes[:, j, :])
             nc.sync.dma_start(first_sb[j][:], first_planes[:, j, :])
 
         ident = keep.tile([P, P], F32, name="ident")
         make_identity(nc, ident[:])
-        size_col = keep.tile([P, PACK], F32, name="size_col")
-        nc.gpsimd.dma_start(size_col[:], size.rearrange("o (p t) -> (o p) t", t=PACK))
 
-        vals_factor = keep.tile([P, PACK], F32, name="vals_factor")
+        vals_factor = keep.tile([P, PACK], F32, name="vals_factor", tag="query_stage", align_bytes=64)
         nc.vector.tensor_tensor(vals_factor[:], lam_col[:], vsc_col[:], ALU.mult)
         neg_first_factor = keep.tile([P, PACK], F32, name="neg_first_factor")
         nc.vector.scalar_tensor_tensor(
             neg_first_factor[:], lam_col[:], 1.0, vsc_col[:], ALU.subtract, ALU.mult
         )
-        factor_rows = []
-        for name, col, sign in (("vals", vals_factor, 1.0), ("first", neg_first_factor, -1.0)):
+
+        def spread_factor(name, col, sign):
             spread = psum2.tile([P, PACK, P], F32, name="turn_ps", tag="turn_ps")
             for t in range(PACK):
                 nc.tensor.transpose(spread[:, t, :], col[:, t : t + 1].to_broadcast([P, P]), ident[:])
@@ -85,31 +84,51 @@ def tile_attend_valueresidual_pl_kernel(
                 ACT.Copy,
                 scale=sign,
             )
-            factor_rows.append(row)
-        vals_row, first_row = factor_rows
+            return row
+
+        vals_row = spread_factor("vals", vals_factor, 1.0)
+        first_row = spread_factor("first", neg_first_factor, -1.0)
 
         key_words_g = keep.tile([P, I], U16, name="key_words_g", align_bytes=64)
         nc.vector.tensor_copy(key_words_g[:], key_words[:].indirect(offsets[:]))
-        key_scales_g = keep.tile([P, I], U8, name="key_scales_g", align_bytes=64)
+        picked_tags = {
+            (0, 1): "query_stage",
+            (1, 0): "sum_stage0",
+            (1, 1): "sum_stage1",
+            (2, 0): "probs1",
+            (2, 1): "inv_sum1",
+        }
+
+        def pick(j, step):
+            pool_sb, row = ((vals_sb[j], vals_row), (first_sb[j], first_row))[step]
+            picked_tag = picked_tags.get((j, step), f"picked{j}_{step}")
+            picked = keep.tile([P, I], F32, name=f"picked{j}_{step}", tag=picked_tag, align_bytes=64)
+            nc.vector.tensor_tensor(picked[:], pool_sb[:].indirect(offsets[:]), row[:], ALU.mult)
+            return picked
+
+        picked_first = pick(0, 0)
+        key_scales_g = keep.tile([P, I], U8, name="key_scales_g", tag="vals_sb0", align_bytes=64)
         nc.vector.tensor_copy(key_scales_g[:], key_scales[:].indirect(offsets[:]))
 
         query_bf = keep.tile([P, Q, PACK], BF16, name="query_bf", tag="query_stage", align_bytes=64)
-        nc.scalar.copy(
-            query_bf[:].rearrange("p (c i) t -> p c t i", i=4),
-            query_sb[:].rearrange("p t (c i) -> p c t i", i=4),
-        )
-        query_codes = keep.tile([P, Q], U32, name="query_codes", align_bytes=64)
+        query_codes = keep.tile([P, Q], U32, name="query_codes", tag="key_scales", align_bytes=64)
         query_scales = keep.tile([P, Q], U8, name="query_scales", align_bytes=64)
-        nc.vector.quantize_mx(
-            out=query_codes[:].bitcast(FP8X4),
-            scales=query_scales[:],
-            in_=query_bf[:].rearrange("p q t -> p (q t)"),
-        )
+        for b in range(Q_BLOCKS):
+            cols = slice(b * P, (b + 1) * P)
+            nc.scalar.copy(
+                query_bf[:, cols, :].rearrange("p (c i) t -> p c t i", i=4),
+                query_sb[:, :, cols].rearrange("p t (c i) -> p c t i", i=4),
+            )
+            nc.vector.quantize_mx(
+                out=query_codes[:, cols].bitcast(FP8X4),
+                scales=query_scales[:, cols],
+                in_=query_bf[:, cols, :].rearrange("p q t -> p (q t)"),
+            )
 
         normed = []
         for b in range(Q_BLOCKS):
             cols = slice(b * P, (b + 1) * P)
-            scores = psum.tile([P, I], F32, name=f"scores{b}")
+            scores = psum.tile([P, I], F32, name=f"scores{b}", tag=f"scores{b}")
             nc.tensor.matmul_mx(
                 out=scores[:],
                 lhsT=query_codes[:, cols].bitcast(FP8X4),
@@ -121,8 +140,8 @@ def tile_attend_valueresidual_pl_kernel(
             )
             neg_max = keep.tile([P, 1], F32, name=f"neg_max{b}")
             nc.vector.tensor_reduce(neg_max[:], scores[:], AXIS_X, ALU.max, negate=True)
-            probs = keep.tile([P, PACK, P], F32, name=f"probs{b}")
-            row_sum = keep.tile([P, 1], F32, name=f"row_sum{b}")
+            probs = keep.tile([P, PACK, P], F32, name=f"probs{b}", tag=f"probs{b}", align_bytes=64)
+            row_sum = keep.tile([P, 1], F32, name=f"row_sum{b}", tag=f"sum_stage{b}", align_bytes=64)
             nc.scalar.activation(
                 probs[:],
                 scores[:].rearrange("q (s t) -> q t s", t=PACK),
@@ -130,9 +149,9 @@ def tile_attend_valueresidual_pl_kernel(
                 bias=neg_max[:],
                 accum_out=row_sum[:],
             )
-            inv_sum = keep.tile([P, 1], F32, name=f"inv_sum{b}")
+            inv_sum = keep.tile([P, 1], F32, name=f"inv_sum{b}", tag=f"inv_sum{b}", align_bytes=64)
             nc.vector.reciprocal(inv_sum[:], row_sum[:])
-            norm = keep.tile([P, PACK, P], F32, name=f"norm{b}")
+            norm = keep.tile([P, PACK, P], F32, name=f"norm{b}", tag=f"norm{b}", align_bytes=64)
             nc.scalar.activation(norm[:], probs[:], ACT.Copy, scale=inv_sum[:])
             normed.append(norm)
 
@@ -154,22 +173,20 @@ def tile_attend_valueresidual_pl_kernel(
             weights_bf[:].rearrange("p (c i) t -> p c t i", i=4),
             weights_planar[:].rearrange("p t (c i) -> p c t i", i=4),
         )
-        weight_codes = keep.tile([P, Q], U32, name="weight_codes", align_bytes=64)
-        weight_scales = keep.tile([P, Q], U8, name="weight_scales", align_bytes=64)
-        nc.vector.quantize_mx(
-            out=weight_codes[:].bitcast(FP8X4),
-            scales=weight_scales[:],
-            in_=weights_bf[:].rearrange("p q t -> p (q t)"),
-        )
 
-        result_ps = [psum.tile([P, PACK, P], F32, name=f"result_ps{b}") for b in range(Q_BLOCKS)]
-        out_planes = out_0.rearrange("(p j) q -> p j q", j=PACK)
+        groups = ((range(0, 2), "norm0"), (range(2, 3), "stage"), (range(3, 4), "value_bf_last"))
+        group_bf = [
+            keep.tile([P, len(planes), P, PACK], BF16, name=f"value_bf{planes.start}", tag=tag, align_bytes=64)
+            for planes, tag in groups
+        ]
+        value_bf = [tile[:, j - planes.start, :, :] for tile, (planes, tag) in zip(group_bf, groups) for j in planes]
         for j in range(PACK):
-            mixed = psum2.tile([P, PACK, P], F32, name="mixed_ps", tag="mixed_ps" if j < 2 else "turn_ps")
-            for step, (pool_sb, row) in enumerate(((vals_sb[j], vals_row), (first_sb[j], first_row))):
-                picked_tag = {(0, 0): "query_stage", (PACK - 1, 1): "stage"}.get((j, step), f"picked{j}_{step}")
-                picked = keep.tile([P, I], F32, name=f"picked{j}_{step}", tag=picked_tag, align_bytes=64)
-                nc.vector.tensor_tensor(picked[:], pool_sb[:].indirect(offsets[:]), row[:], ALU.mult)
+            if j < 2:
+                mixed = psum2.tile([P, PACK, P], F32, name="mixed_ps", tag="mixed_ps")
+            else:
+                mixed = psum.tile([P, PACK, P], F32, name="mixed_ps", tag=f"scores{j - 2}")
+            for step in range(2):
+                picked = picked_first if (j, step) == (0, 0) else pick(j, step)
                 by_place = picked[:].rearrange("e (s t) -> e t s", t=PACK)
                 for t in range(PACK):
                     nc.tensor.matmul(
@@ -180,38 +197,51 @@ def tile_attend_valueresidual_pl_kernel(
                         stop=(step == 1 and t == PACK - 1),
                         is_transpose=True,
                     )
-            value_bf = keep.tile(
-                [P, P, PACK], BF16, name=f"value_bf{j}", tag="stage" if j == 1 else f"value_bf{j}", align_bytes=64
-            )
-            nc.scalar.copy(value_bf[:], mixed[:].rearrange("s t m -> s m t"))
-            value_codes = keep.tile([P, P], U32, name=f"value_codes{j}", align_bytes=64)
-            value_scales = keep.tile([P, P], U8, name=f"value_scales{j}", align_bytes=64)
-            nc.vector.quantize_mx(
-                out=value_codes[:].bitcast(FP8X4),
-                scales=value_scales[:],
-                in_=value_bf[:].rearrange("s m t -> s (m t)"),
-            )
-            result = keep.tile([P, Q], F32, name=f"result{j}")
-            for b in range(Q_BLOCKS):
-                cols = slice(b * P, (b + 1) * P)
-                nc.tensor.matmul_mx(
-                    out=result_ps[b][:, j, :],
-                    lhsT=value_codes[:].bitcast(FP8X4),
-                    lhsT_scale=value_scales[:],
-                    rhs=weight_codes[:, cols].bitcast(FP8X4),
-                    rhs_scale=weight_scales[:, cols],
-                    start=True,
-                    stop=True,
-                )
-            if j == PACK - 1:
-                result_bf = keep.tile([P, Q, PACK], BF16, name="result_bf", align_bytes=64)
-                nc.vector.tensor_copy(result_bf[:, 0:P, :], result_ps[0][:].rearrange("p j q -> p q j"))
-                nc.scalar.copy(result_bf[:, P:Q, :], result_ps[1][:].rearrange("p j q -> p q j"))
-            for b in reversed(range(Q_BLOCKS)):
-                cols = slice(b * P, (b + 1) * P)
-                nc.scalar.copy(result[:, cols], result_ps[b][:, j, :])
-            nc.sync.dma_start(out_planes[:, j, :], result[:])
+            nc.scalar.copy(value_bf[j], mixed[:].rearrange("s t m -> s m t"))
 
+        codes = keep.tile([P, Q + PACK * P], U32, name="codes", tag=f"first_sb{PACK - 1}", align_bytes=64)
+        weight_codes = codes[:, 0:Q]
+        weight_scales = keep.tile([P, Q], U8, name="weight_scales", align_bytes=64)
+        nc.vector.quantize_mx(
+            out=weight_codes.bitcast(FP8X4),
+            scales=weight_scales[:],
+            in_=weights_bf[:].rearrange("p q t -> p (q t)"),
+        )
+        value_scales = keep.tile([P, PACK * P], U8, name="value_scales", align_bytes=64)
+        result_ps = [psum.tile([P, PACK, P], F32, name=f"result_ps{b}") for b in range(Q_BLOCKS)]
+        result = keep.tile([P, PACK, Q], F32, name="result")
+        result_bf = keep.tile([P, Q, PACK], BF16, name="result_bf", align_bytes=64)
+        out_planes = out_0.rearrange("(p j) q -> p j q", j=PACK)
+        for tile, (planes, tag) in zip(group_bf, groups):
+            lo, hi = planes.start, planes.stop
+            nc.vector.quantize_mx(
+                out=codes[:, Q + lo * P : Q + hi * P].bitcast(FP8X4),
+                scales=value_scales[:, lo * P : hi * P],
+                in_=tile[:].rearrange("s j m t -> s (j m t)"),
+            )
+            for j in planes:
+                for b in range(Q_BLOCKS):
+                    cols = slice(b * P, (b + 1) * P)
+                    nc.tensor.matmul_mx(
+                        out=result_ps[b][:, j, :],
+                        lhsT=codes[:, Q + j * P : Q + (j + 1) * P].bitcast(FP8X4),
+                        lhsT_scale=value_scales[:, j * P : (j + 1) * P],
+                        rhs=weight_codes[:, cols].bitcast(FP8X4),
+                        rhs_scale=weight_scales[:, cols],
+                        start=True,
+                        stop=True,
+                    )
+            if hi == PACK - 1:
+                nc.vector.tensor_copy(result[:, 0:hi, 0:P], result_ps[0][:, 0:hi, :])
+                nc.scalar.copy(result[:, 0:hi, P:Q], result_ps[1][:, 0:hi, :])
+                nc.sync.dma_start(out_planes[:, 0:hi, :], result[:, 0:hi, :])
+
+        last = PACK - 1
+        nc.vector.tensor_copy(result_bf[:, 0:P, :], result_ps[0][:].rearrange("p j q -> p q j"))
+        nc.scalar.copy(result_bf[:, P:Q, :], result_ps[1][:].rearrange("p j q -> p q j"))
+        for b in reversed(range(Q_BLOCKS)):
+            nc.scalar.copy(result[:, last, b * P : (b + 1) * P], result_ps[b][:, last, :])
+        nc.sync.dma_start(out_planes[:, last, :], result[:, last, :])
         result_codes = keep.tile([P, Q], U32, name="result_codes", align_bytes=64)
         result_scales = keep.tile([P, Q], U8, name="result_scales", align_bytes=64)
         nc.vector.quantize_mx(

@@ -35,7 +35,7 @@ def tile_attend_valueresidual_pl_kernel(
         offsets = keep.tile([P, I // 16], U16, name="offsets")
         nc.sync.dma_start(offsets[:], offs)
 
-        key_scales = keep.tile([P, T], U8, name="key_scales", tag="key_scales", align_bytes=64)
+        key_scales = keep.tile([P, T], U8, name="key_scales", align_bytes=64)
         nc.gpsimd.memset(key_scales[:].bitcast(I32), 0)
 
         lam_col = keep.tile([P, PACK], F32, name="lam_col")
@@ -46,10 +46,10 @@ def tile_attend_valueresidual_pl_kernel(
         nc.sync.dma_start(key_words[:].bitcast(I32), keys_words[0].bitcast(I32))
         vals_planes = vals.rearrange("(p j) n -> p j n", j=PACK)
         first_planes = first.rearrange("(p j) n -> p j n", j=PACK)
-        vals_sb = [keep.tile([P, T], F32, name=f"vals_sb{j}", tag=f"vals_sb{j}", align_bytes=64) for j in range(PACK)]
+        vals_sb = [keep.tile([P, T], F32, name=f"vals_sb{j}") for j in range(PACK)]
         first_sb = [keep.tile([P, T], F32, name=f"first_sb{j}", tag=f"first_sb{j}", align_bytes=64) for j in range(PACK)]
         nc.sync.dma_start(vals_sb[0][:], vals_planes[:, 0, :])
-        query_sb = keep.tile([P, PACK, Q], F32, name="query_sb")
+        query_sb = keep.tile([P, PACK, Q], F32, name="query_sb", tag="query_raw", align_bytes=64)
         nc.sync.dma_start(query_sb[:], query.rearrange("(p j) q -> p j q", j=PACK))
         for quad in range(4):
             nc.sync.dma_start(
@@ -87,16 +87,18 @@ def tile_attend_valueresidual_pl_kernel(
             return row
 
         vals_row = spread_factor("vals", vals_factor, 1.0)
-        first_row = spread_factor("first", neg_first_factor, -1.0)
+        minus_one = keep.tile([P, 1], F32, name="minus_one", tag="minus_one", align_bytes=64)
+        nc.gpsimd.memset(minus_one[:], -1.0)
+        first_row = spread_factor("first", neg_first_factor, minus_one[:])
 
-        key_words_g = keep.tile([P, I], U16, name="key_words_g", align_bytes=64)
+        key_words_g = keep.tile([P, I], U16, name="key_words_g", tag="key_words_g", align_bytes=64)
         nc.vector.tensor_copy(key_words_g[:], key_words[:].indirect(offsets[:]))
         picked_tags = {
-            (0, 1): "query_stage",
-            (1, 0): "sum_stage0",
-            (1, 1): "sum_stage1",
+            (0, 1): "query_raw",
+            (1, 0): "key_words_g",
+            (1, 1): "neg_max1",
             (2, 0): "probs1",
-            (2, 1): "inv_sum1",
+            (2, 1): "inv_sums",
         }
 
         def pick(j, step):
@@ -107,11 +109,11 @@ def tile_attend_valueresidual_pl_kernel(
             return picked
 
         picked_first = pick(0, 0)
-        key_scales_g = keep.tile([P, I], U8, name="key_scales_g", tag="vals_sb0", align_bytes=64)
+        key_scales_g = keep.tile([P, I], U8, name="key_scales_g", tag="minus_one", align_bytes=64)
         nc.vector.tensor_copy(key_scales_g[:], key_scales[:].indirect(offsets[:]))
 
         query_bf = keep.tile([P, Q, PACK], BF16, name="query_bf", tag="query_stage", align_bytes=64)
-        query_codes = keep.tile([P, Q], U32, name="query_codes", tag="key_scales", align_bytes=64)
+        query_codes = keep.tile([P, Q], U32, name="query_codes", align_bytes=64)
         query_scales = keep.tile([P, Q], U8, name="query_scales", align_bytes=64)
         for b in range(Q_BLOCKS):
             cols = slice(b * P, (b + 1) * P)
@@ -125,7 +127,8 @@ def tile_attend_valueresidual_pl_kernel(
                 in_=query_bf[:, cols, :].rearrange("p q t -> p (q t)"),
             )
 
-        normed = []
+        row_sums = keep.tile([P, Q_BLOCKS], F32, name="row_sums")
+        all_probs = []
         for b in range(Q_BLOCKS):
             cols = slice(b * P, (b + 1) * P)
             scores = psum.tile([P, I], F32, name=f"scores{b}", tag=f"scores{b}")
@@ -138,43 +141,41 @@ def tile_attend_valueresidual_pl_kernel(
                 start=True,
                 stop=True,
             )
-            neg_max = keep.tile([P, 1], F32, name=f"neg_max{b}")
+            neg_max = keep.tile([P, 1], F32, name=f"neg_max{b}", tag=f"neg_max{b}", align_bytes=64)
             nc.vector.tensor_reduce(neg_max[:], scores[:], AXIS_X, ALU.max, negate=True)
             probs = keep.tile([P, PACK, P], F32, name=f"probs{b}", tag=f"probs{b}", align_bytes=64)
-            row_sum = keep.tile([P, 1], F32, name=f"row_sum{b}", tag=f"sum_stage{b}", align_bytes=64)
             nc.scalar.activation(
                 probs[:],
                 scores[:].rearrange("q (s t) -> q t s", t=PACK),
                 ACT.Exp,
                 bias=neg_max[:],
-                accum_out=row_sum[:],
+                accum_out=row_sums[:, b : b + 1],
             )
-            inv_sum = keep.tile([P, 1], F32, name=f"inv_sum{b}", tag=f"inv_sum{b}", align_bytes=64)
-            nc.vector.reciprocal(inv_sum[:], row_sum[:])
-            norm = keep.tile([P, PACK, P], F32, name=f"norm{b}", tag=f"norm{b}", align_bytes=64)
-            nc.scalar.activation(norm[:], probs[:], ACT.Copy, scale=inv_sum[:])
+            all_probs.append(probs)
+        inv_sums = keep.tile([P, Q_BLOCKS], F32, name="inv_sums", tag="inv_sums", align_bytes=64)
+        nc.vector.reciprocal(inv_sums[:], row_sums[:])
+        normed = []
+        for b in range(Q_BLOCKS):
+            norm = keep.tile([P, PACK, P], F32, name=f"norm{b}")
+            nc.scalar.activation(norm[:], all_probs[b][:], ACT.Copy, scale=inv_sums[:, b : b + 1])
             normed.append(norm)
 
         weights_planar = keep.tile([P, PACK, Q], BF16, name="weights_planar", tag="stage", align_bytes=64)
-        for half in range(2):
-            turned = psum2.tile([P, 2, Q], F32, name="turn_ps", tag="turn_ps")
-            for u in range(2):
-                for b in range(Q_BLOCKS):
-                    nc.tensor.transpose(
-                        turned[:, u, b * P : (b + 1) * P], normed[b][:, 2 * half + u, :], ident[:]
-                    )
-            for u in range(2):
-                t = 2 * half + u
-                nc.scalar.activation(
-                    weights_planar[:, t, :], turned[:, u, :], ACT.Copy, scale=size_col[:, t : t + 1]
-                )
+        turned = [psum2.tile([P, 2, Q], F32, name="turn_ps", tag="turn_ps") for half in range(2)]
+        for b in range(Q_BLOCKS):
+            for t in range(PACK):
+                nc.tensor.transpose(turned[t // 2][:, t % 2, b * P : (b + 1) * P], normed[b][:, t, :], ident[:])
+        for t in range(PACK):
+            nc.scalar.activation(
+                weights_planar[:, t, :], turned[t // 2][:, t % 2, :], ACT.Copy, scale=size_col[:, t : t + 1]
+            )
         weights_bf = keep.tile([P, Q, PACK], BF16, name="weights_bf", align_bytes=64)
         nc.scalar.copy(
             weights_bf[:].rearrange("p (c i) t -> p c t i", i=4),
             weights_planar[:].rearrange("p t (c i) -> p c t i", i=4),
         )
 
-        groups = ((range(0, 2), "norm0"), (range(2, 3), "stage"), (range(3, 4), "value_bf_last"))
+        groups = ((range(0, 2), "neg_max0"), (range(2, 3), "stage"), (range(3, 4), "value_bf_last"))
         group_bf = [
             keep.tile([P, len(planes), P, PACK], BF16, name=f"value_bf{planes.start}", tag=tag, align_bytes=64)
             for planes, tag in groups

@@ -21,6 +21,10 @@ AXIS_X = mybir.AxisListType.X
 P = 128
 PACK = 4
 Q_BLOCKS = Q // P
+QUADRANTS = 4
+SCALE_ROWS = 4
+WALK = 4
+VALS, FIRST = 0, 1
 
 
 def tile_attend_valueresidual_pl_kernel(
@@ -47,14 +51,16 @@ def tile_attend_valueresidual_pl_kernel(
         vals_planes = vals.rearrange("(p j) n -> p j n", j=PACK)
         first_planes = first.rearrange("(p j) n -> p j n", j=PACK)
         vals_sb = [keep.tile([P, T], F32, name=f"vals_sb{j}") for j in range(PACK)]
-        first_sb = [keep.tile([P, T], F32, name=f"first_sb{j}", tag=f"first_sb{j}", align_bytes=64) for j in range(PACK)]
+        first_sb = [
+            keep.tile([P, T], F32, name=f"first_sb{j}", tag=f"first_sb{j}", align_bytes=64) for j in range(PACK)
+        ]
         nc.sync.dma_start(vals_sb[0][:], vals_planes[:, 0, :])
         query_sb = keep.tile([P, PACK, Q], F32, name="query_sb", tag="query_raw", align_bytes=64)
         nc.sync.dma_start(query_sb[:], query.rearrange("(p j) q -> p j q", j=PACK))
-        for quad in range(4):
+        for quad in range(QUADRANTS):
             nc.sync.dma_start(
-                key_scales[32 * quad : 32 * quad + 4, :].bitcast(I32),
-                keys_scales[0, 4 * quad : 4 * quad + 4, :].bitcast(I32),
+                key_scales[32 * quad : 32 * quad + SCALE_ROWS, :].bitcast(I32),
+                keys_scales[0, SCALE_ROWS * quad : SCALE_ROWS * (quad + 1), :].bitcast(I32),
             )
         nc.sync.dma_start(first_sb[0][:], first_planes[:, 0, :])
         size_col = keep.tile([P, PACK], F32, name="size_col")
@@ -93,22 +99,23 @@ def tile_attend_valueresidual_pl_kernel(
 
         key_words_g = keep.tile([P, I], U16, name="key_words_g", tag="key_words_g", align_bytes=64)
         nc.vector.tensor_copy(key_words_g[:], key_words[:].indirect(offsets[:]))
+
         picked_tags = {
-            (0, 1): "query_raw",
-            (1, 0): "key_words_g",
-            (1, 1): "neg_max1",
-            (2, 0): "probs1",
-            (2, 1): "inv_sums",
+            (0, FIRST): "query_raw",
+            (1, VALS): "key_words_g",
+            (1, FIRST): "neg_max1",
+            (2, VALS): "probs0",
+            (2, FIRST): "probs1",
         }
 
-        def pick(j, step):
-            pool_sb, row = ((vals_sb[j], vals_row), (first_sb[j], first_row))[step]
-            picked_tag = picked_tags.get((j, step), f"picked{j}_{step}")
-            picked = keep.tile([P, I], F32, name=f"picked{j}_{step}", tag=picked_tag, align_bytes=64)
+        def pick(j, pool):
+            pool_sb, row = ((vals_sb[j], vals_row), (first_sb[j], first_row))[pool]
+            picked_tag = picked_tags.get((j, pool), f"picked{j}_{pool}")
+            picked = keep.tile([P, I], F32, name=f"picked{j}_{pool}", tag=picked_tag, align_bytes=64)
             nc.vector.tensor_tensor(picked[:], pool_sb[:].indirect(offsets[:]), row[:], ALU.mult)
             return picked
 
-        picked_first = pick(0, 0)
+        vals_plane_0 = pick(0, VALS)
         key_scales_g = keep.tile([P, I], U8, name="key_scales_g", tag="minus_one", align_bytes=64)
         nc.vector.tensor_copy(key_scales_g[:], key_scales[:].indirect(offsets[:]))
 
@@ -118,8 +125,8 @@ def tile_attend_valueresidual_pl_kernel(
         for b in range(Q_BLOCKS):
             cols = slice(b * P, (b + 1) * P)
             nc.scalar.copy(
-                query_bf[:, cols, :].rearrange("p (c i) t -> p c t i", i=4),
-                query_sb[:, :, cols].rearrange("p t (c i) -> p c t i", i=4),
+                query_bf[:, cols, :].rearrange("p (c i) t -> p c t i", i=WALK),
+                query_sb[:, :, cols].rearrange("p t (c i) -> p c t i", i=WALK),
             )
             nc.vector.quantize_mx(
                 out=query_codes[:, cols].bitcast(FP8X4),
@@ -131,7 +138,7 @@ def tile_attend_valueresidual_pl_kernel(
         all_probs = []
         for b in range(Q_BLOCKS):
             cols = slice(b * P, (b + 1) * P)
-            scores = psum.tile([P, I], F32, name=f"scores{b}", tag=f"scores{b}")
+            scores = psum.tile([P, I], F32, name=f"scores{b}")
             nc.tensor.matmul_mx(
                 out=scores[:],
                 lhsT=query_codes[:, cols].bitcast(FP8X4),
@@ -152,7 +159,7 @@ def tile_attend_valueresidual_pl_kernel(
                 accum_out=row_sums[:, b : b + 1],
             )
             all_probs.append(probs)
-        inv_sums = keep.tile([P, Q_BLOCKS], F32, name="inv_sums", tag="inv_sums", align_bytes=64)
+        inv_sums = keep.tile([P, Q_BLOCKS], F32, name="inv_sums")
         nc.vector.reciprocal(inv_sums[:], row_sums[:])
         normed = []
         for b in range(Q_BLOCKS):
@@ -171,36 +178,34 @@ def tile_attend_valueresidual_pl_kernel(
             )
         weights_bf = keep.tile([P, Q, PACK], BF16, name="weights_bf", align_bytes=64)
         nc.scalar.copy(
-            weights_bf[:].rearrange("p (c i) t -> p c t i", i=4),
-            weights_planar[:].rearrange("p t (c i) -> p c t i", i=4),
+            weights_bf[:].rearrange("p (c i) t -> p c t i", i=WALK),
+            weights_planar[:].rearrange("p t (c i) -> p c t i", i=WALK),
         )
 
-        groups = ((range(0, 2), "neg_max0"), (range(2, 3), "stage"), (range(3, 4), "value_bf_last"))
+        last = PACK - 1
+        groups = ((range(0, 2), "neg_max0"), (range(2, last), "stage"), (range(last, PACK), "value_bf_last"))
         group_bf = [
             keep.tile([P, len(planes), P, PACK], BF16, name=f"value_bf{planes.start}", tag=tag, align_bytes=64)
             for planes, tag in groups
         ]
         value_bf = [tile[:, j - planes.start, :, :] for tile, (planes, tag) in zip(group_bf, groups) for j in planes]
         for j in range(PACK):
-            if j < 2:
-                mixed = psum2.tile([P, PACK, P], F32, name="mixed_ps", tag="mixed_ps")
-            else:
-                mixed = psum.tile([P, PACK, P], F32, name="mixed_ps", tag=f"scores{j - 2}")
-            for step in range(2):
-                picked = picked_first if (j, step) == (0, 0) else pick(j, step)
+            mixed = psum2.tile([P, PACK, P], F32, name="mixed_ps", tag="mixed_ps" if j < 2 else "turn_ps")
+            for pool in (VALS, FIRST):
+                picked = vals_plane_0 if (j, pool) == (0, VALS) else pick(j, pool)
                 by_place = picked[:].rearrange("e (s t) -> e t s", t=PACK)
                 for t in range(PACK):
                     nc.tensor.matmul(
                         mixed[:, t, :],
                         by_place[:, t, :],
                         ident[:],
-                        start=(step == 0 and t == 0),
-                        stop=(step == 1 and t == PACK - 1),
+                        start=(pool == VALS and t == 0),
+                        stop=(pool == FIRST and t == PACK - 1),
                         is_transpose=True,
                     )
             nc.scalar.copy(value_bf[j], mixed[:].rearrange("s t m -> s m t"))
 
-        codes = keep.tile([P, Q + PACK * P], U32, name="codes", tag=f"first_sb{PACK - 1}", align_bytes=64)
+        codes = keep.tile([P, Q + PACK * P], U32, name="codes", tag=f"first_sb{last}", align_bytes=64)
         weight_codes = codes[:, 0:Q]
         weight_scales = keep.tile([P, Q], U8, name="weight_scales", align_bytes=64)
         nc.vector.quantize_mx(
@@ -232,12 +237,11 @@ def tile_attend_valueresidual_pl_kernel(
                         start=True,
                         stop=True,
                     )
-            if hi == PACK - 1:
+            if hi == last:
                 nc.vector.tensor_copy(result[:, 0:hi, 0:P], result_ps[0][:, 0:hi, :])
                 nc.scalar.copy(result[:, 0:hi, P:Q], result_ps[1][:, 0:hi, :])
                 nc.sync.dma_start(out_planes[:, 0:hi, :], result[:, 0:hi, :])
 
-        last = PACK - 1
         nc.vector.tensor_copy(result_bf[:, 0:P, :], result_ps[0][:].rearrange("p j q -> p q j"))
         nc.scalar.copy(result_bf[:, P:Q, :], result_ps[1][:].rearrange("p j q -> p q j"))
         for b in reversed(range(Q_BLOCKS)):
@@ -253,9 +257,9 @@ def tile_attend_valueresidual_pl_kernel(
         nc.sync.dma_start(
             out_1[0].rearrange("p q j -> p (q j)").bitcast(I32), result_codes[:].bitcast(I32)
         )
-        for quad in range(4):
+        for quad in range(QUADRANTS):
             queue = nc.scalar if quad % 2 == 0 else nc.sync
             queue.dma_start(
-                out_2[0, 4 * quad : 4 * quad + 4, :].bitcast(I32),
-                result_scales[32 * quad : 32 * quad + 4, :].bitcast(I32),
+                out_2[0, SCALE_ROWS * quad : SCALE_ROWS * (quad + 1), :].bitcast(I32),
+                result_scales[32 * quad : 32 * quad + SCALE_ROWS, :].bitcast(I32),
             )

@@ -33,6 +33,7 @@ def tile_attend_valueresidual_pl_kernel(
     nc = tc.nc
     with ExitStack() as ctx:
         keep = ctx.enter_context(tc.tile_pool(name="keep", bufs=1))
+        shared = ctx.enter_context(tc.tile_pool(name="shared", bufs=1))
         psum = ctx.enter_context(tc.psum_pool(name="psum", bufs=1))
         psum2 = ctx.enter_context(tc.psum_pool(name="psum2", bufs=2))
 
@@ -54,14 +55,14 @@ def tile_attend_valueresidual_pl_kernel(
         first_sb = [
             keep.tile([P, T], F32, name=f"first_sb{j}", tag=f"first_sb{j}", align_bytes=64) for j in range(PACK)
         ]
-        nc.sync.dma_start(vals_sb[0][:], vals_planes[:, 0, :])
-        query_sb = keep.tile([P, PACK, Q], F32, name="query_sb", tag="query_raw", align_bytes=64)
+        query_sb = shared.tile([P, PACK, Q], F32, name="query_sb", offset=0, align_bytes=64)
         nc.sync.dma_start(query_sb[:], query.rearrange("(p j) q -> p j q", j=PACK))
         for quad in range(QUADRANTS):
             nc.sync.dma_start(
                 key_scales[32 * quad : 32 * quad + SCALE_ROWS, :].bitcast(I32),
                 keys_scales[0, SCALE_ROWS * quad : SCALE_ROWS * (quad + 1), :].bitcast(I32),
             )
+        nc.sync.dma_start(vals_sb[0][:], vals_planes[:, 0, :])
         nc.sync.dma_start(first_sb[0][:], first_planes[:, 0, :])
         size_col = keep.tile([P, PACK], F32, name="size_col")
         nc.sync.dma_start(size_col[:], size.rearrange("o (p t) -> (o p) t", t=PACK))
@@ -72,54 +73,49 @@ def tile_attend_valueresidual_pl_kernel(
         ident = keep.tile([P, P], F32, name="ident")
         make_identity(nc, ident[:])
 
-        vals_factor = keep.tile([P, PACK], F32, name="vals_factor", tag="query_stage", align_bytes=64)
+        vals_factor = keep.tile([P, PACK], F32, name="vals_factor")
         nc.vector.tensor_tensor(vals_factor[:], lam_col[:], vsc_col[:], ALU.mult)
         neg_first_factor = keep.tile([P, PACK], F32, name="neg_first_factor")
         nc.vector.scalar_tensor_tensor(
             neg_first_factor[:], lam_col[:], 1.0, vsc_col[:], ALU.subtract, ALU.mult
         )
 
-        def spread_factor(name, col, sign):
+        def spread_factor(row, col, sign):
             spread = psum2.tile([P, PACK, P], F32, name="turn_ps", tag="turn_ps")
             for t in range(PACK):
                 nc.tensor.transpose(spread[:, t, :], col[:, t : t + 1].to_broadcast([P, P]), ident[:])
-            row = keep.tile([P, I], F32, name=f"{name}_row")
             nc.scalar.activation(
                 row[:].rearrange("m (p t) -> m p t", t=PACK),
                 spread[:].rearrange("m t p -> m p t"),
                 ACT.Copy,
                 scale=sign,
             )
-            return row
 
-        vals_row = spread_factor("vals", vals_factor, 1.0)
-        minus_one = keep.tile([P, 1], F32, name="minus_one", tag="minus_one", align_bytes=64)
-        nc.gpsimd.memset(minus_one[:], -1.0)
-        first_row = spread_factor("first", neg_first_factor, minus_one[:])
+        vals_row = keep.tile([P, I], F32, name="vals_row")
+        spread_factor(vals_row, vals_factor, 1.0)
 
         key_words_g = keep.tile([P, I], U16, name="key_words_g", tag="key_words_g", align_bytes=64)
         nc.vector.tensor_copy(key_words_g[:], key_words[:].indirect(offsets[:]))
 
         picked_tags = {
-            (0, FIRST): "query_raw",
-            (1, VALS): "key_words_g",
-            (1, FIRST): "neg_max1",
-            (2, VALS): "probs0",
-            (2, FIRST): "probs1",
+            (0, FIRST): "key_words_g",
+            (1, VALS): "neg_max1",
         }
 
         def pick(j, pool):
             pool_sb, row = ((vals_sb[j], vals_row), (first_sb[j], first_row))[pool]
             picked_tag = picked_tags.get((j, pool), f"picked{j}_{pool}")
-            picked = keep.tile([P, I], F32, name=f"picked{j}_{pool}", tag=picked_tag, align_bytes=64)
+            if (j, pool) == (0, VALS):
+                picked = shared.tile([P, I], F32, name="picked0_0", offset=0, align_bytes=64)
+            else:
+                picked = keep.tile([P, I], F32, name=f"picked{j}_{pool}", tag=picked_tag, align_bytes=64)
             nc.vector.tensor_tensor(picked[:], pool_sb[:].indirect(offsets[:]), row[:], ALU.mult)
             return picked
 
-        vals_plane_0 = pick(0, VALS)
-        key_scales_g = keep.tile([P, I], U8, name="key_scales_g", tag="minus_one", align_bytes=64)
+        key_scales_g = keep.tile([P, I], U8, name="key_scales_g", align_bytes=64)
         nc.vector.tensor_copy(key_scales_g[:], key_scales[:].indirect(offsets[:]))
 
-        query_bf = keep.tile([P, Q, PACK], BF16, name="query_bf", tag="query_stage", align_bytes=64)
+        query_bf = keep.tile([P, Q, PACK], BF16, name="query_bf", align_bytes=64)
         query_codes = keep.tile([P, Q], U32, name="query_codes", align_bytes=64)
         query_scales = keep.tile([P, Q], U8, name="query_scales", align_bytes=64)
         for b in range(Q_BLOCKS):
@@ -128,17 +124,19 @@ def tile_attend_valueresidual_pl_kernel(
                 query_bf[:, cols, :].rearrange("p (c i) t -> p c t i", i=WALK),
                 query_sb[:, :, cols].rearrange("p t (c i) -> p c t i", i=WALK),
             )
-            nc.vector.quantize_mx(
-                out=query_codes[:, cols].bitcast(FP8X4),
-                scales=query_scales[:, cols],
-                in_=query_bf[:, cols, :].rearrange("p q t -> p (q t)"),
-            )
+        nc.vector.quantize_mx(
+            out=query_codes[:].bitcast(FP8X4),
+            scales=query_scales[:],
+            in_=query_bf[:].rearrange("p q t -> p (q t)"),
+        )
+        first_row = shared.tile([P, I], F32, name="first_row", offset=4 * I, align_bytes=64)
+        spread_factor(first_row, neg_first_factor, -1.0)
 
         row_sums = keep.tile([P, Q_BLOCKS], F32, name="row_sums")
         all_probs = []
         for b in range(Q_BLOCKS):
             cols = slice(b * P, (b + 1) * P)
-            scores = psum.tile([P, I], F32, name=f"scores{b}")
+            scores = psum.tile([P, I], F32, name=f"scores{b}", tag=f"scores{b}")
             nc.tensor.matmul_mx(
                 out=scores[:],
                 lhsT=query_codes[:, cols].bitcast(FP8X4),
@@ -183,16 +181,17 @@ def tile_attend_valueresidual_pl_kernel(
         )
 
         last = PACK - 1
-        groups = ((range(0, 2), "neg_max0"), (range(2, last), "stage"), (range(last, PACK), "value_bf_last"))
+        groups = ((range(0, 2), "probs0"), (range(2, last), "stage"), (range(last, PACK), "value_bf_last"))
         group_bf = [
             keep.tile([P, len(planes), P, PACK], BF16, name=f"value_bf{planes.start}", tag=tag, align_bytes=64)
             for planes, tag in groups
         ]
         value_bf = [tile[:, j - planes.start, :, :] for tile, (planes, tag) in zip(group_bf, groups) for j in planes]
         for j in range(PACK):
-            mixed = psum2.tile([P, PACK, P], F32, name="mixed_ps", tag="mixed_ps" if j < 2 else "turn_ps")
+            mixed = psum.tile([P, PACK, P], F32, name="mixed_ps", tag="mixed_ps" if j < 2 else f"scores{j - 2}")
             for pool in (VALS, FIRST):
-                picked = vals_plane_0 if (j, pool) == (0, VALS) else pick(j, pool)
+                picked = pick(j, pool)
+                last_picked = picked
                 by_place = picked[:].rearrange("e (s t) -> e t s", t=PACK)
                 for t in range(PACK):
                     nc.tensor.matmul(

@@ -191,12 +191,19 @@ def tile_attend_valueresidual_pl_kernel(
             mixed = psum.tile([P, PACK, P], F32, name="mixed_ps", tag="mixed_ps" if j < 2 else f"scores{j - 2}")
             for pool in (VALS, FIRST):
                 picked = pick(j, pool)
-                last_picked = picked
                 by_place = picked[:].rearrange("e (s t) -> e t s", t=PACK)
+                places = [by_place[:, t, :] for t in range(PACK)]
+                if (j, pool) == (last, FIRST):
+                    laid = keep.tile([P, 2, P], F32, name="laid")
+                    nc.scalar.copy(
+                        laid[:].rearrange("e t s -> e s t"),
+                        picked[:].rearrange("e (s t) -> e s t", t=PACK)[:, :, 2:PACK],
+                    )
+                    places[2:PACK] = [laid[:, 0, :], laid[:, 1, :]]
                 for t in range(PACK):
                     nc.tensor.matmul(
                         mixed[:, t, :],
-                        by_place[:, t, :],
+                        places[t],
                         ident[:],
                         start=(pool == VALS and t == 0),
                         stop=(pool == FIRST and t == PACK - 1),
@@ -245,7 +252,7 @@ def tile_attend_valueresidual_pl_kernel(
         nc.scalar.copy(result_bf[:, P:Q, :], result_ps[1][:].rearrange("p j q -> p q j"))
         for b in reversed(range(Q_BLOCKS)):
             nc.scalar.copy(result[:, last, b * P : (b + 1) * P], result_ps[b][:, last, :])
-        nc.sync.dma_start(out_planes[:, last, :], result[:, last, :])
+        nc.scalar.dma_start(out_planes[:, last, :], result[:, last, :])
         result_codes = keep.tile([P, Q], U32, name="result_codes", align_bytes=64)
         result_scales = keep.tile([P, Q], U8, name="result_scales", align_bytes=64)
         nc.vector.quantize_mx(

@@ -224,34 +224,42 @@ def tile_attend_valueresidual_pl_kernel(
         result = keep.tile([P, PACK, Q], F32, name="result")
         result_bf = keep.tile([P, Q, PACK], BF16, name="result_bf", align_bytes=64)
         out_planes = out_0.rearrange("(p j) q -> p j q", j=PACK)
-        for tile, (planes, tag) in zip(group_bf, groups):
-            lo, hi = planes.start, planes.stop
+
+        def quantise_values(tile, planes):
             nc.vector.quantize_mx(
-                out=codes[:, Q + lo * P : Q + hi * P].bitcast(FP8X4),
-                scales=value_scales[:, lo * P : hi * P],
+                out=codes[:, Q + planes.start * P : Q + planes.stop * P].bitcast(FP8X4),
+                scales=value_scales[:, planes.start * P : planes.stop * P],
                 in_=tile[:].rearrange("s j m t -> s (j m t)"),
             )
-            for j in planes:
-                for b in range(Q_BLOCKS):
-                    cols = slice(b * P, (b + 1) * P)
-                    nc.tensor.matmul_mx(
-                        out=result_ps[b][:, j, :],
-                        lhsT=codes[:, Q + j * P : Q + (j + 1) * P].bitcast(FP8X4),
-                        lhsT_scale=value_scales[:, j * P : (j + 1) * P],
-                        rhs=weight_codes[:, cols].bitcast(FP8X4),
-                        rhs_scale=weight_scales[:, cols],
-                        start=True,
-                        stop=True,
-                    )
-            if hi == last:
-                nc.vector.tensor_copy(result[:, 0:hi, 0:P], result_ps[0][:, 0:hi, :])
-                nc.scalar.copy(result[:, 0:hi, P:Q], result_ps[1][:, 0:hi, :])
-                nc.sync.dma_start(out_planes[:, 0:hi, :], result[:, 0:hi, :])
+
+        def multiply(j, b):
+            cols = slice(b * P, (b + 1) * P)
+            nc.tensor.matmul_mx(
+                out=result_ps[b][:, j, :],
+                lhsT=codes[:, Q + j * P : Q + (j + 1) * P].bitcast(FP8X4),
+                lhsT_scale=value_scales[:, j * P : (j + 1) * P],
+                rhs=weight_codes[:, cols].bitcast(FP8X4),
+                rhs_scale=weight_scales[:, cols],
+                start=True,
+                stop=True,
+            )
+
+        for tile, (planes, tag) in zip(group_bf[:-1], groups[:-1]):
+            quantise_values(tile, planes)
+        for b in range(Q_BLOCKS):
+            for j in range(last):
+                multiply(j, b)
+        nc.vector.tensor_copy(result[:, 0:last, 0:P], result_ps[0][:, 0:last, :])
+        nc.scalar.copy(result[:, 0:last, P:Q], result_ps[1][:, 0:last, :])
+        nc.sync.dma_start(out_planes[:, 0:last, :], result[:, 0:last, :])
+        quantise_values(group_bf[-1], groups[-1][0])
+        for b in range(Q_BLOCKS):
+            multiply(last, b)
 
         nc.vector.tensor_copy(result_bf[:, 0:P, :], result_ps[0][:].rearrange("p j q -> p q j"))
         nc.scalar.copy(result_bf[:, P:Q, :], result_ps[1][:].rearrange("p j q -> p q j"))
-        for b in reversed(range(Q_BLOCKS)):
-            nc.scalar.copy(result[:, last, b * P : (b + 1) * P], result_ps[b][:, last, :])
+        nc.vector.tensor_copy(result[:, last, 0:P], result_ps[0][:, last, :])
+        nc.scalar.copy(result[:, last, P:Q], result_ps[1][:, last, :])
         nc.scalar.dma_start(out_planes[:, last, :], result[:, last, :])
         result_codes = keep.tile([P, Q], U32, name="result_codes", align_bytes=64)
         result_scales = keep.tile([P, Q], U8, name="result_scales", align_bytes=64)

@@ -188,7 +188,14 @@ def tile_attend_valueresidual_pl_kernel(
         ]
         value_bf = [tile[:, j - planes.start, :, :] for tile, (planes, tag) in zip(group_bf, groups) for j in planes]
         for j in range(PACK):
-            mixed = psum.tile([P, PACK, P], F32, name="mixed_ps", tag="mixed_ps" if j < 2 else f"scores{j - 2}")
+            if j < last:
+                mixed = psum.tile([P, PACK, P], F32, name="mixed_ps", tag="mixed_ps" if j < 2 else "scores0")
+                targets = [mixed[:, t, :] for t in range(PACK)]
+                per_bank = PACK
+            else:
+                halves = [psum.tile([P, 2, P], F32, name="half_ps", tag=tag) for tag in ("scores1", "half_ps")]
+                targets = [halves[t // 2][:, t % 2, :] for t in range(PACK)]
+                per_bank = 2
             for pool in (VALS, FIRST):
                 picked = pick(j, pool)
                 by_place = picked[:].rearrange("e (s t) -> e t s", t=PACK)
@@ -202,14 +209,17 @@ def tile_attend_valueresidual_pl_kernel(
                     places[2:PACK] = [laid[:, 0, :], laid[:, 1, :]]
                 for t in range(PACK):
                     nc.tensor.matmul(
-                        mixed[:, t, :],
+                        targets[t],
                         places[t],
                         ident[:],
-                        start=(pool == VALS and t == 0),
-                        stop=(pool == FIRST and t == PACK - 1),
+                        start=(pool == VALS and t % per_bank == 0),
+                        stop=(pool == FIRST and t % per_bank == per_bank - 1),
                         is_transpose=True,
                     )
-            nc.scalar.copy(value_bf[j], mixed[:].rearrange("s t m -> s m t"))
+            if j < last:
+                nc.scalar.copy(value_bf[j], mixed[:].rearrange("s t m -> s m t"))
+            else:
+                nc.scalar.copy(value_bf[j][:, :, 2:PACK], halves[1][:].rearrange("s t m -> s m t"))
 
         codes = keep.tile([P, Q + PACK * P], U32, name="codes", tag=f"first_sb{last}", align_bytes=64)
         weight_codes = codes[:, 0:Q]
@@ -232,10 +242,9 @@ def tile_attend_valueresidual_pl_kernel(
                 in_=tile[:].rearrange("s j m t -> s (j m t)"),
             )
 
-        def multiply(j, b):
-            cols = slice(b * P, (b + 1) * P)
+        def multiply(j, cols, bank):
             nc.tensor.matmul_mx(
-                out=result_ps[b][:, j, :],
+                out=bank,
                 lhsT=codes[:, Q + j * P : Q + (j + 1) * P].bitcast(FP8X4),
                 lhsT_scale=value_scales[:, j * P : (j + 1) * P],
                 rhs=weight_codes[:, cols].bitcast(FP8X4),
@@ -246,15 +255,21 @@ def tile_attend_valueresidual_pl_kernel(
 
         for tile, (planes, tag) in zip(group_bf[:-1], groups[:-1]):
             quantise_values(tile, planes)
+        nc.vector.tensor_copy(value_bf[last][:, :, 0:2], halves[0][:].rearrange("s t m -> s m t"))
+        blocks = [slice(b * P, (b + 1) * P) for b in range(Q_BLOCKS)]
         for b in range(Q_BLOCKS):
-            for j in range(last):
-                multiply(j, b)
-        nc.vector.tensor_copy(result[:, 0:last, 0:P], result_ps[0][:, 0:last, :])
-        nc.scalar.copy(result[:, 0:last, P:Q], result_ps[1][:, 0:last, :])
+            for j in range(2):
+                multiply(j, blocks[b], result_ps[b][:, j, :])
+        plane_2_ps = psum.tile([P, Q], F32, name="plane_2_ps", tag="mixed_ps")
+        multiply(2, slice(0, Q), plane_2_ps[:])
+        nc.vector.tensor_copy(result[:, 0:2, 0:P], result_ps[0][:, 0:2, :])
+        nc.scalar.copy(result[:, 0:2, P:Q], result_ps[1][:, 0:2, :])
+        nc.scalar.copy(result[:, 2, :], plane_2_ps[:])
         nc.sync.dma_start(out_planes[:, 0:last, :], result[:, 0:last, :])
         quantise_values(group_bf[-1], groups[-1][0])
         for b in range(Q_BLOCKS):
-            multiply(last, b)
+            for j in range(2, PACK):
+                multiply(j, blocks[b], result_ps[b][:, j, :])
 
         nc.vector.tensor_copy(result_bf[:, 0:P, :], result_ps[0][:].rearrange("p j q -> p q j"))
         nc.scalar.copy(result_bf[:, P:Q, :], result_ps[1][:].rearrange("p j q -> p q j"))

@@ -278,14 +278,14 @@ def tile_attend_valueresidual_pl_kernel(
         nc.scalar.dma_start(out_planes[:, last, :], result[:, last, :])
         result_codes = keep.tile([P, Q], U32, name="result_codes", align_bytes=64)
         result_scales = keep.tile([P, Q], U8, name="result_scales", align_bytes=64)
-        nc.vector.quantize_mx(
-            out=result_codes[:].bitcast(FP8X4),
-            scales=result_scales[:],
-            in_=result_bf[:].rearrange("p q j -> p (q j)"),
-        )
-        nc.sync.dma_start(
-            out_1[0].rearrange("p q j -> p (q j)").bitcast(I32), result_codes[:].bitcast(I32)
-        )
+        out_words = out_1[0].rearrange("p q j -> p (q j)").bitcast(I32)
+        for cols in blocks:
+            nc.vector.quantize_mx(
+                out=result_codes[:, cols].bitcast(FP8X4),
+                scales=result_scales[:, cols],
+                in_=result_bf[:, cols, :].rearrange("p q j -> p (q j)"),
+            )
+            nc.sync.dma_start(out_words[:, cols], result_codes[:, cols].bitcast(I32))
         for quad in range(QUADRANTS):
             queue = nc.scalar if quad % 2 == 0 else nc.sync
             queue.dma_start(

@@ -45,8 +45,6 @@ def tile_attend_valueresidual_pl_kernel(
 
         lam_col = keep.tile([P, PACK], F32, name="lam_col")
         nc.sync.dma_start(lam_col[:], lam.rearrange("o (p t) -> (o p) t", t=PACK))
-        vsc_col = keep.tile([P, PACK], F32, name="vsc_col")
-        nc.sync.dma_start(vsc_col[:], vsc.rearrange("(p t) o -> p (t o)", t=PACK))
         key_words = keep.tile([P, T], U16, name="key_words", align_bytes=64)
         nc.sync.dma_start(key_words[:].bitcast(I32), keys_words[0].bitcast(I32))
         vals_planes = vals.rearrange("(p j) n -> p j n", j=PACK)
@@ -55,13 +53,15 @@ def tile_attend_valueresidual_pl_kernel(
         first_sb = [
             keep.tile([P, T], F32, name=f"first_sb{j}", tag=f"first_sb{j}", align_bytes=64) for j in range(PACK)
         ]
-        query_sb = shared.tile([P, PACK, Q], F32, name="query_sb", offset=0, align_bytes=64)
-        nc.sync.dma_start(query_sb[:], query.rearrange("(p j) q -> p j q", j=PACK))
         for quad in range(QUADRANTS):
             nc.sync.dma_start(
                 key_scales[32 * quad : 32 * quad + SCALE_ROWS, :].bitcast(I32),
                 keys_scales[0, SCALE_ROWS * quad : SCALE_ROWS * (quad + 1), :].bitcast(I32),
             )
+        query_sb = shared.tile([P, PACK, Q], F32, name="query_sb", offset=0, align_bytes=64)
+        nc.sync.dma_start(query_sb[:], query.rearrange("(p j) q -> p j q", j=PACK))
+        vsc_col = keep.tile([P, PACK], F32, name="vsc_col")
+        nc.sync.dma_start(vsc_col[:], vsc.rearrange("(p t) o -> p (t o)", t=PACK))
         nc.sync.dma_start(vals_sb[0][:], vals_planes[:, 0, :])
         nc.sync.dma_start(first_sb[0][:], first_planes[:, 0, :])
         size_col = keep.tile([P, PACK], F32, name="size_col")
@@ -74,25 +74,18 @@ def tile_attend_valueresidual_pl_kernel(
         make_identity(nc, ident[:])
 
         vals_factor = keep.tile([P, PACK], F32, name="vals_factor")
-        nc.vector.tensor_tensor(vals_factor[:], lam_col[:], vsc_col[:], ALU.mult)
-        neg_first_factor = keep.tile([P, PACK], F32, name="neg_first_factor")
-        nc.vector.scalar_tensor_tensor(
-            neg_first_factor[:], lam_col[:], 1.0, vsc_col[:], ALU.subtract, ALU.mult
-        )
+        nc.gpsimd.tensor_tensor(vals_factor[:], lam_col[:], vsc_col[:], ALU.mult)
+        first_share = keep.tile([P, PACK], F32, name="first_share")
+        nc.gpsimd.tensor_scalar(first_share[:], lam_col[:], -1.0, 1.0, ALU.mult, ALU.add)
+        first_factor = keep.tile([P, PACK], F32, name="first_factor")
+        nc.gpsimd.tensor_tensor(first_factor[:], first_share[:], vsc_col[:], ALU.mult)
 
-        def spread_factor(row, col, sign):
+        def spread_factor(row, col):
             spread = psum2.tile([P, PACK, P], F32, name="turn_ps", tag="turn_ps")
             for t in range(PACK):
                 nc.tensor.transpose(spread[:, t, :], col[:, t : t + 1].to_broadcast([P, P]), ident[:])
-            nc.scalar.activation(
-                row[:].rearrange("m (p t) -> m p t", t=PACK),
-                spread[:].rearrange("m t p -> m p t"),
-                ACT.Copy,
-                scale=sign,
-            )
+            nc.scalar.copy(row[:].rearrange("m (p t) -> m p t", t=PACK), spread[:].rearrange("m t p -> m p t"))
 
-        vals_row = keep.tile([P, I], F32, name="vals_row")
-        spread_factor(vals_row, vals_factor, 1.0)
 
         key_words_g = keep.tile([P, I], U16, name="key_words_g", tag="key_words_g", align_bytes=64)
         nc.vector.tensor_copy(key_words_g[:], key_words[:].indirect(offsets[:]))
@@ -106,10 +99,17 @@ def tile_attend_valueresidual_pl_kernel(
             pool_sb, row = ((vals_sb[j], vals_row), (first_sb[j], first_row))[pool]
             picked_tag = picked_tags.get((j, pool), f"picked{j}_{pool}")
             if (j, pool) == (0, VALS):
-                picked = shared.tile([P, I], F32, name="picked0_0", offset=0, align_bytes=64)
+                half = I // 2
+                plain = shared.tile([P, half], F32, name="plain", offset=0, align_bytes=64)
+                picked = keep.tile([P, I], F32, name="picked0_0")
+                nc.vector.tensor_copy(plain[:], pool_sb[:].indirect(offsets[:, 0 : half // 16]))
+                nc.vector.tensor_tensor(
+                    picked[:, half:I], pool_sb[:].indirect(offsets[:, half // 16 : I // 16]), row[:, half:I], ALU.mult
+                )
+                nc.gpsimd.tensor_tensor(picked[:, 0:half], plain[:], row[:, 0:half], ALU.mult)
             else:
                 picked = keep.tile([P, I], F32, name=f"picked{j}_{pool}", tag=picked_tag, align_bytes=64)
-            nc.vector.tensor_tensor(picked[:], pool_sb[:].indirect(offsets[:]), row[:], ALU.mult)
+                nc.vector.tensor_tensor(picked[:], pool_sb[:].indirect(offsets[:]), row[:], ALU.mult)
             return picked
 
         key_scales_g = keep.tile([P, I], U8, name="key_scales_g", align_bytes=64)
@@ -129,8 +129,10 @@ def tile_attend_valueresidual_pl_kernel(
             scales=query_scales[:],
             in_=query_bf[:].rearrange("p q t -> p (q t)"),
         )
+        vals_row = keep.tile([P, I], F32, name="vals_row")
+        spread_factor(vals_row, vals_factor)
         first_row = shared.tile([P, I], F32, name="first_row", offset=4 * I, align_bytes=64)
-        spread_factor(first_row, neg_first_factor, -1.0)
+        spread_factor(first_row, first_factor)
 
         row_sums = keep.tile([P, Q_BLOCKS], F32, name="row_sums")
         all_probs = []
@@ -278,14 +280,14 @@ def tile_attend_valueresidual_pl_kernel(
         nc.scalar.dma_start(out_planes[:, last, :], result[:, last, :])
         result_codes = keep.tile([P, Q], U32, name="result_codes", align_bytes=64)
         result_scales = keep.tile([P, Q], U8, name="result_scales", align_bytes=64)
-        out_words = out_1[0].rearrange("p q j -> p (q j)").bitcast(I32)
-        for cols in blocks:
-            nc.vector.quantize_mx(
-                out=result_codes[:, cols].bitcast(FP8X4),
-                scales=result_scales[:, cols],
-                in_=result_bf[:, cols, :].rearrange("p q j -> p (q j)"),
-            )
-            nc.sync.dma_start(out_words[:, cols], result_codes[:, cols].bitcast(I32))
+        nc.vector.quantize_mx(
+            out=result_codes[:].bitcast(FP8X4),
+            scales=result_scales[:],
+            in_=result_bf[:].rearrange("p q j -> p (q j)"),
+        )
+        nc.sync.dma_start(
+            out_1[0].rearrange("p q j -> p (q j)").bitcast(I32), result_codes[:].bitcast(I32)
+        )
         for quad in range(QUADRANTS):
             queue = nc.scalar if quad % 2 == 0 else nc.sync
             queue.dma_start(

@@ -232,7 +232,8 @@ def tile_attend_valueresidual_pl_kernel(
             in_=weights_bf[:].rearrange("p q t -> p (q t)"),
         )
         value_scales = keep.tile([P, PACK * P], U8, name="value_scales", align_bytes=64)
-        result_ps = [psum.tile([P, PACK, P], F32, name=f"result_ps{b}") for b in range(Q_BLOCKS)]
+        early_ps = [psum2.tile([P, 2, P], F32, name="turn_ps", tag="turn_ps") for b in range(Q_BLOCKS)]
+        late_ps = [psum.tile([P, 2, P], F32, name=f"late_ps{b}") for b in range(Q_BLOCKS)]
         result = keep.tile([P, PACK, Q], F32, name="result")
         result_bf = keep.tile([P, Q, PACK], BF16, name="result_bf", align_bytes=64)
         out_planes = out_0.rearrange("(p j) q -> p j q", j=PACK)
@@ -261,22 +262,27 @@ def tile_attend_valueresidual_pl_kernel(
         blocks = [slice(b * P, (b + 1) * P) for b in range(Q_BLOCKS)]
         for b in range(Q_BLOCKS):
             for j in range(2):
-                multiply(j, blocks[b], result_ps[b][:, j, :])
+                multiply(j, blocks[b], early_ps[b][:, j, :])
+        for b in range(Q_BLOCKS):
+            multiply(2, blocks[b], late_ps[b][:, 0, :])
         plane_2_ps = psum.tile([P, Q], F32, name="plane_2_ps", tag="mixed_ps")
         multiply(2, slice(0, Q), plane_2_ps[:])
-        nc.vector.tensor_copy(result[:, 0:2, 0:P], result_ps[0][:, 0:2, :])
-        nc.scalar.copy(result[:, 0:2, P:Q], result_ps[1][:, 0:2, :])
-        nc.scalar.copy(result[:, 2, :], plane_2_ps[:])
-        nc.sync.dma_start(out_planes[:, 0:last, :], result[:, 0:last, :])
         quantise_values(group_bf[-1], groups[-1][0])
         for b in range(Q_BLOCKS):
-            for j in range(2, PACK):
-                multiply(j, blocks[b], result_ps[b][:, j, :])
+            multiply(last, blocks[b], late_ps[b][:, 1, :])
+        for b in range(Q_BLOCKS):
+            nc.scalar.copy(result[:, 0:2, blocks[b]], early_ps[b][:])
+        nc.vector.tensor_copy(result_bf[:, 0:P, 0:2], result[:, 0:2, 0:P].rearrange("p j q -> p q j"))
+        nc.gpsimd.tensor_scalar(
+            result_bf[:, P:Q, 0:2], result[:, 0:2, P:Q].rearrange("p j q -> p q j"), 1.0, 0.0, ALU.mult, ALU.add
+        )
+        nc.scalar.copy(result[:, 2, :], plane_2_ps[:])
+        nc.sync.dma_start(out_planes[:, 0:last, :], result[:, 0:last, :])
 
-        nc.vector.tensor_copy(result_bf[:, 0:P, :], result_ps[0][:].rearrange("p j q -> p q j"))
-        nc.scalar.copy(result_bf[:, P:Q, :], result_ps[1][:].rearrange("p j q -> p q j"))
-        nc.vector.tensor_copy(result[:, last, 0:P], result_ps[0][:, last, :])
-        nc.scalar.copy(result[:, last, P:Q], result_ps[1][:, last, :])
+        nc.vector.tensor_copy(result_bf[:, 0:P, 2:PACK], late_ps[0][:].rearrange("p j q -> p q j"))
+        nc.scalar.copy(result_bf[:, P:Q, 2:PACK], late_ps[1][:].rearrange("p j q -> p q j"))
+        nc.vector.tensor_copy(result[:, last, 0:P], late_ps[0][:, 1, :])
+        nc.scalar.copy(result[:, last, P:Q], late_ps[1][:, 1, :])
         nc.scalar.dma_start(out_planes[:, last, :], result[:, last, :])
         result_codes = keep.tile([P, Q], U32, name="result_codes", align_bytes=64)
         result_scales = keep.tile([P, Q], U8, name="result_scales", align_bytes=64)

@@ -202,13 +202,6 @@ def tile_attend_valueresidual_pl_kernel(
                 picked = pick(j, pool)
                 by_place = picked[:].rearrange("e (s t) -> e t s", t=PACK)
                 places = [by_place[:, t, :] for t in range(PACK)]
-                if (j, pool) == (last, FIRST):
-                    laid = keep.tile([P, 2, P], F32, name="laid")
-                    nc.scalar.copy(
-                        laid[:].rearrange("e t s -> e s t"),
-                        picked[:].rearrange("e (s t) -> e s t", t=PACK)[:, :, 2:PACK],
-                    )
-                    places[2:PACK] = [laid[:, 0, :], laid[:, 1, :]]
                 for t in range(PACK):
                     nc.tensor.matmul(
                         targets[t],

@@ -269,14 +269,14 @@ def tile_attend_valueresidual_pl_kernel(
         nc.gpsimd.tensor_scalar(
             result_bf[:, P:Q, 0:2], result[:, 0:2, P:Q].rearrange("p j q -> p q j"), 1.0, 0.0, ALU.mult, ALU.add
         )
+        nc.sync.dma_start(out_planes[:, 0:2, :], result[:, 0:2, :])
         nc.scalar.copy(result[:, 2, :], plane_2_ps[:])
-        nc.sync.dma_start(out_planes[:, 0:last, :], result[:, 0:last, :])
 
         nc.vector.tensor_copy(result_bf[:, 0:P, 2:PACK], late_ps[0][:].rearrange("p j q -> p q j"))
         nc.scalar.copy(result_bf[:, P:Q, 2:PACK], late_ps[1][:].rearrange("p j q -> p q j"))
         nc.vector.tensor_copy(result[:, last, 0:P], late_ps[0][:, 1, :])
         nc.scalar.copy(result[:, last, P:Q], late_ps[1][:, 1, :])
-        nc.scalar.dma_start(out_planes[:, last, :], result[:, last, :])
+        nc.scalar.dma_start(out_planes[:, 2:PACK, :], result[:, 2:PACK, :])
         result_codes = keep.tile([P, Q], U32, name="result_codes", align_bytes=64)
         result_scales = keep.tile([P, Q], U8, name="result_scales", align_bytes=64)
         nc.vector.quantize_mx(

@@ -25,6 +25,7 @@ QUADRANTS = 4
 SCALE_ROWS = 4
 WALK = 4
 VALS, FIRST = 0, 1
+TINY = 2.0**-60
 
 
 def tile_attend_valueresidual_pl_kernel(
@@ -33,9 +34,10 @@ def tile_attend_valueresidual_pl_kernel(
     nc = tc.nc
     with ExitStack() as ctx:
         keep = ctx.enter_context(tc.tile_pool(name="keep", bufs=1))
-        shared = ctx.enter_context(tc.tile_pool(name="shared", bufs=1))
         psum = ctx.enter_context(tc.psum_pool(name="psum", bufs=1))
-        psum2 = ctx.enter_context(tc.psum_pool(name="psum2", bufs=2))
+
+        def bank(k, shape, name):
+            return psum.tile(shape, F32, name=name, tag=f"bank{k}")
 
         offsets = keep.tile([P, I // 16], U16, name="offsets")
         nc.sync.dma_start(offsets[:], offs)
@@ -47,71 +49,48 @@ def tile_attend_valueresidual_pl_kernel(
         nc.sync.dma_start(lam_col[:], lam.rearrange("o (p t) -> (o p) t", t=PACK))
         key_words = keep.tile([P, T], U16, name="key_words", align_bytes=64)
         nc.sync.dma_start(key_words[:].bitcast(I32), keys_words[0].bitcast(I32))
-        vals_planes = vals.rearrange("(p j) n -> p j n", j=PACK)
-        first_planes = first.rearrange("(p j) n -> p j n", j=PACK)
-        vals_sb = [keep.tile([P, T], F32, name=f"vals_sb{j}") for j in range(PACK)]
-        first_sb = [
-            keep.tile([P, T], F32, name=f"first_sb{j}", tag=f"first_sb{j}", align_bytes=64) for j in range(PACK)
-        ]
         for quad in range(QUADRANTS):
             nc.sync.dma_start(
                 key_scales[32 * quad : 32 * quad + SCALE_ROWS, :].bitcast(I32),
                 keys_scales[0, SCALE_ROWS * quad : SCALE_ROWS * (quad + 1), :].bitcast(I32),
             )
-        query_sb = shared.tile([P, PACK, Q], F32, name="query_sb", offset=0, align_bytes=64)
+        query_sb = keep.tile([P, PACK, Q], F32, name="query_sb", tag="query_sb", align_bytes=64)
         nc.sync.dma_start(query_sb[:], query.rearrange("(p j) q -> p j q", j=PACK))
+        planes_hbm = (vals.rearrange("(p j) n -> p j n", j=PACK), first.rearrange("(p j) n -> p j n", j=PACK))
+        pool_sb = {}
+
+        def load(j, pool):
+            pool_sb[j, pool] = keep.tile([P, T], F32, name=f"pool{j}_{pool}", align_bytes=64)
+            nc.sync.dma_start(pool_sb[j, pool][:], planes_hbm[pool][:, j, :])
+
+        load(0, VALS)
+        load(0, FIRST)
+        load(1, VALS)
         vsc_col = keep.tile([P, PACK], F32, name="vsc_col")
         nc.sync.dma_start(vsc_col[:], vsc.rearrange("(p t) o -> p (t o)", t=PACK))
-        nc.sync.dma_start(vals_sb[0][:], vals_planes[:, 0, :])
-        nc.sync.dma_start(first_sb[0][:], first_planes[:, 0, :])
-        size_col = keep.tile([P, PACK], F32, name="size_col")
+        size_col = keep.tile([P, PACK], F32, name="size_col", align_bytes=64)
         nc.sync.dma_start(size_col[:], size.rearrange("o (p t) -> (o p) t", t=PACK))
-        for j in range(1, PACK):
-            nc.sync.dma_start(vals_sb[j][:], vals_planes[:, j, :])
-            nc.sync.dma_start(first_sb[j][:], first_planes[:, j, :])
+        for j, pool in ((2, VALS), (1, FIRST), (3, VALS), (2, FIRST), (3, FIRST)):
+            load(j, pool)
 
         ident = keep.tile([P, P], F32, name="ident")
         make_identity(nc, ident[:])
 
-        vals_factor = keep.tile([P, PACK], F32, name="vals_factor")
-        nc.gpsimd.tensor_tensor(vals_factor[:], lam_col[:], vsc_col[:], ALU.mult)
-        first_share = keep.tile([P, PACK], F32, name="first_share")
-        nc.gpsimd.tensor_scalar(first_share[:], lam_col[:], -1.0, 1.0, ALU.mult, ALU.add)
-        first_factor = keep.tile([P, PACK], F32, name="first_factor")
-        nc.gpsimd.tensor_tensor(first_factor[:], first_share[:], vsc_col[:], ALU.mult)
+        neg_share = keep.tile([P, PACK], F32, name="neg_share")
+        nc.vector.tensor_scalar(neg_share[:], lam_col[:], 1.0, TINY, ALU.subtract, ALU.subtract)
+        neg_inverse = keep.tile([P, PACK], F32, name="neg_inverse")
+        nc.vector.reciprocal(neg_inverse[:], neg_share[:])
+        neg_ratio = keep.tile([P, PACK], F32, name="neg_ratio")
+        nc.gpsimd.tensor_tensor(neg_ratio[:], lam_col[:], neg_inverse[:], ALU.mult)
+        share = keep.tile([P, PACK], F32, name="share")
+        nc.gpsimd.tensor_scalar(share[:], neg_share[:], -1.0, 0.0, ALU.mult, ALU.add)
 
-        def spread_factor(row, col):
-            spread = psum2.tile([P, PACK, P], F32, name="turn_ps", tag="turn_ps")
-            for t in range(PACK):
-                nc.tensor.transpose(spread[:, t, :], col[:, t : t + 1].to_broadcast([P, P]), ident[:])
-            nc.scalar.copy(row[:].rearrange("m (p t) -> m p t", t=PACK), spread[:].rearrange("m t p -> m p t"))
+        spread = bank(2, [P, PACK, P], "spread")
+        for t in range(PACK):
+            nc.tensor.transpose(spread[:, t, :], neg_ratio[:, t : t + 1].to_broadcast([P, P]), ident[:])
 
-
-        key_words_g = keep.tile([P, I], U16, name="key_words_g", tag="key_words_g", align_bytes=64)
+        key_words_g = keep.tile([P, I], U16, name="key_words_g", align_bytes=64)
         nc.vector.tensor_copy(key_words_g[:], key_words[:].indirect(offsets[:]))
-
-        picked_tags = {
-            (0, FIRST): "key_words_g",
-            (1, VALS): "neg_max1",
-        }
-
-        def pick(j, pool):
-            pool_sb, row = ((vals_sb[j], vals_row), (first_sb[j], first_row))[pool]
-            picked_tag = picked_tags.get((j, pool), f"picked{j}_{pool}")
-            if (j, pool) == (0, VALS):
-                half = I // 2
-                plain = shared.tile([P, half], F32, name="plain", offset=0, align_bytes=64)
-                picked = keep.tile([P, I], F32, name="picked0_0")
-                nc.vector.tensor_copy(plain[:], pool_sb[:].indirect(offsets[:, 0 : half // 16]))
-                nc.vector.tensor_tensor(
-                    picked[:, half:I], pool_sb[:].indirect(offsets[:, half // 16 : I // 16]), row[:, half:I], ALU.mult
-                )
-                nc.gpsimd.tensor_tensor(picked[:, 0:half], plain[:], row[:, 0:half], ALU.mult)
-            else:
-                picked = keep.tile([P, I], F32, name=f"picked{j}_{pool}", tag=picked_tag, align_bytes=64)
-                nc.vector.tensor_tensor(picked[:], pool_sb[:].indirect(offsets[:]), row[:], ALU.mult)
-            return picked
-
         key_scales_g = keep.tile([P, I], U8, name="key_scales_g", align_bytes=64)
         nc.vector.tensor_copy(key_scales_g[:], key_scales[:].indirect(offsets[:]))
 
@@ -124,21 +103,27 @@ def tile_attend_valueresidual_pl_kernel(
                 query_bf[:, cols, :].rearrange("p (c i) t -> p c t i", i=WALK),
                 query_sb[:, :, cols].rearrange("p t (c i) -> p c t i", i=WALK),
             )
-        nc.vector.quantize_mx(
-            out=query_codes[:].bitcast(FP8X4),
-            scales=query_scales[:],
-            in_=query_bf[:].rearrange("p q t -> p (q t)"),
-        )
-        vals_row = keep.tile([P, I], F32, name="vals_row")
-        spread_factor(vals_row, vals_factor)
-        first_row = shared.tile([P, I], F32, name="first_row", offset=4 * I, align_bytes=64)
-        spread_factor(first_row, first_factor)
+            nc.vector.quantize_mx(
+                out=query_codes[:, cols].bitcast(FP8X4),
+                scales=query_scales[:, cols],
+                in_=query_bf[:, cols, :].rearrange("p q t -> p (q t)"),
+            )
 
-        row_sums = keep.tile([P, Q_BLOCKS], F32, name="row_sums")
+        ratio_row = keep.tile([P, I], F32, name="ratio_row", tag="query_sb", align_bytes=64)
+        nc.vector.tensor_scalar(
+            ratio_row[:].rearrange("m (p t) -> m p t", t=PACK),
+            spread[:].rearrange("m t p -> m p t"),
+            -1.0,
+            0.0,
+            ALU.mult,
+            ALU.add,
+        )
+
+        row_sums = keep.tile([P, Q_BLOCKS], F32, name="row_sums", align_bytes=64)
         all_probs = []
         for b in range(Q_BLOCKS):
             cols = slice(b * P, (b + 1) * P)
-            scores = psum.tile([P, I], F32, name=f"scores{b}", tag=f"scores{b}")
+            scores = bank(b, [P, I], f"scores{b}")
             nc.tensor.matmul_mx(
                 out=scores[:],
                 lhsT=query_codes[:, cols].bitcast(FP8X4),
@@ -148,9 +133,9 @@ def tile_attend_valueresidual_pl_kernel(
                 start=True,
                 stop=True,
             )
-            neg_max = keep.tile([P, 1], F32, name=f"neg_max{b}", tag=f"neg_max{b}", align_bytes=64)
+            neg_max = keep.tile([P, 1], F32, name=f"neg_max{b}", align_bytes=64)
             nc.vector.tensor_reduce(neg_max[:], scores[:], AXIS_X, ALU.max, negate=True)
-            probs = keep.tile([P, PACK, P], F32, name=f"probs{b}", tag=f"probs{b}", align_bytes=64)
+            probs = keep.tile([P, PACK, P], F32, name=f"probs{b}", align_bytes=64)
             nc.scalar.activation(
                 probs[:],
                 scores[:].rearrange("q (s t) -> q t s", t=PACK),
@@ -161,87 +146,108 @@ def tile_attend_valueresidual_pl_kernel(
             all_probs.append(probs)
         inv_sums = keep.tile([P, Q_BLOCKS], F32, name="inv_sums")
         nc.vector.reciprocal(inv_sums[:], row_sums[:])
-        normed = []
-        for b in range(Q_BLOCKS):
-            norm = keep.tile([P, PACK, P], F32, name=f"norm{b}")
-            nc.scalar.activation(norm[:], all_probs[b][:], ACT.Copy, scale=inv_sums[:, b : b + 1])
-            normed.append(norm)
-
-        weights_planar = keep.tile([P, PACK, Q], BF16, name="weights_planar", tag="stage", align_bytes=64)
-        turned = [psum2.tile([P, 2, Q], F32, name="turn_ps", tag="turn_ps") for half in range(2)]
-        for b in range(Q_BLOCKS):
-            for t in range(PACK):
-                nc.tensor.transpose(turned[t // 2][:, t % 2, b * P : (b + 1) * P], normed[b][:, t, :], ident[:])
-        for t in range(PACK):
-            nc.scalar.activation(
-                weights_planar[:, t, :], turned[t // 2][:, t % 2, :], ACT.Copy, scale=size_col[:, t : t + 1]
-            )
         weights_bf = keep.tile([P, Q, PACK], BF16, name="weights_bf", align_bytes=64)
-        nc.scalar.copy(
-            weights_bf[:].rearrange("p (c i) t -> p c t i", i=WALK),
-            weights_planar[:].rearrange("p t (c i) -> p c t i", i=WALK),
-        )
+        for b in range(Q_BLOCKS):
+            norm = keep.tile([P, PACK, P], F32, name=f"norm{b}", align_bytes=64)
+            nc.scalar.activation(norm[:], all_probs[b][:], ACT.Copy, scale=inv_sums[:, b : b + 1])
+            turned = bank(b, [P, PACK, P], f"turned{b}")
+            for t in range(PACK):
+                nc.tensor.transpose(turned[:, t, :], norm[:, t, :], ident[:])
+            nc.vector.tensor_tensor(
+                weights_bf[:, b * P : (b + 1) * P, :],
+                turned[:].rearrange("s t q -> s q t"),
+                size_col[:].unsqueeze(1).to_broadcast([P, P, PACK]),
+                ALU.mult,
+            )
+
+        picked_tags = {
+            (1, VALS): "key_words_g",
+            (2, VALS): "neg_max1",
+            (3, VALS): "norm1",
+            (1, FIRST): "row_sums",
+        }
+
+        def pick(j, pool):
+            tag = picked_tags.get((j, pool), f"picked{j}_{pool}")
+            picked = keep.tile([P, I], F32, name=f"picked{j}_{pool}", tag=tag, align_bytes=64)
+            listed = pool_sb[j, pool][:].indirect(offsets[:])
+            if pool == FIRST:
+                nc.scalar.activation(picked[:], listed, ACT.Copy)
+            elif j == 0:
+                plain = keep.tile([P, I], F32, name="plain")
+                for half in range(2):
+                    cols = slice(half * I // 2, (half + 1) * I // 2)
+                    listed = pool_sb[j, pool][:].indirect(offsets[:, cols.start // 16 : cols.stop // 16])
+                    nc.scalar.activation(plain[:, cols], listed, ACT.Copy)
+                    nc.gpsimd.tensor_tensor(picked[:, cols], plain[:, cols], ratio_row[:, cols], ALU.mult)
+            else:
+                nc.vector.tensor_tensor(picked[:], listed, ratio_row[:], ALU.mult)
+            return picked
 
         last = PACK - 1
-        groups = ((range(0, 2), "probs0"), (range(2, last), "stage"), (range(last, PACK), "value_bf_last"))
-        group_bf = [
-            keep.tile([P, len(planes), P, PACK], BF16, name=f"value_bf{planes.start}", tag=tag, align_bytes=64)
-            for planes, tag in groups
-        ]
-        value_bf = [tile[:, j - planes.start, :, :] for tile, (planes, tag) in zip(group_bf, groups) for j in planes]
+        value_tags = ("probs0", "value_bf1", "value_bf2", f"value_bf{last}")
+        mixed_banks = (2, 3, 4, 5)
+        all_mixed = []
         for j in range(PACK):
-            if j < last:
-                mixed = psum.tile([P, PACK, P], F32, name="mixed_ps", tag="mixed_ps" if j < 2 else "scores0")
-                targets = [mixed[:, t, :] for t in range(PACK)]
-                per_bank = PACK
-            else:
-                halves = [psum.tile([P, 2, P], F32, name="half_ps", tag=tag) for tag in ("scores1", "half_ps")]
-                targets = [halves[t // 2][:, t % 2, :] for t in range(PACK)]
-                per_bank = 2
+            mixed = bank(mixed_banks[j], [P, PACK, P], f"mixed{j}")
+            all_mixed.append(mixed)
             for pool in (VALS, FIRST):
-                picked = pick(j, pool)
-                by_place = picked[:].rearrange("e (s t) -> e t s", t=PACK)
-                places = [by_place[:, t, :] for t in range(PACK)]
+                by_place = pick(j, pool)[:].rearrange("e (s t) -> e t s", t=PACK)
                 for t in range(PACK):
                     nc.tensor.matmul(
-                        targets[t],
-                        places[t],
+                        mixed[:, t, :],
+                        by_place[:, t, :],
                         ident[:],
-                        start=(pool == VALS and t % per_bank == 0),
-                        stop=(pool == FIRST and t % per_bank == per_bank - 1),
+                        start=(pool == VALS and t == 0),
+                        stop=(pool == FIRST and t == PACK - 1),
                         is_transpose=True,
                     )
-            if j < last:
-                nc.scalar.copy(value_bf[j], mixed[:].rearrange("s t m -> s m t"))
-            else:
-                nc.scalar.copy(value_bf[j][:, :, 2:PACK], halves[1][:].rearrange("s t m -> s m t"))
+            if j == 0:
+                outer = keep.tile([P, PACK], F32, name="outer", tag="plain")
+                nc.gpsimd.tensor_tensor(outer[:], share[:], vsc_col[:], ALU.mult)
 
-        codes = keep.tile([P, Q + PACK * P], U32, name="codes", tag=f"first_sb{last}", align_bytes=64)
-        weight_codes = codes[:, 0:Q]
+        value_bf = []
+
+        def round_values(j):
+            tile = keep.tile([P, P, PACK], BF16, name=f"value_bf{j}", tag=value_tags[j], align_bytes=64)
+            nc.vector.tensor_tensor(
+                tile[:],
+                all_mixed[j][:].rearrange("s t m -> s m t"),
+                outer[:].unsqueeze(1).to_broadcast([P, P, PACK]),
+                ALU.mult,
+            )
+            value_bf.append(tile)
+
+        round_values(0)
+        round_values(1)
+        weight_codes = keep.tile([P, Q], U32, name="weight_codes", align_bytes=64)
         weight_scales = keep.tile([P, Q], U8, name="weight_scales", align_bytes=64)
         nc.vector.quantize_mx(
-            out=weight_codes.bitcast(FP8X4),
+            out=weight_codes[:].bitcast(FP8X4),
             scales=weight_scales[:],
             in_=weights_bf[:].rearrange("p q t -> p (q t)"),
         )
+
+        early_codes = keep.tile([P, 2 * P], U32, name="early_codes", align_bytes=64)
+        late_codes = keep.tile([P, 2 * P], U32, name="late_codes", tag=f"picked{last}_{FIRST}", align_bytes=64)
+        value_codes = [(early_codes, late_codes)[j // 2][:, j % 2 * P : (j % 2 + 1) * P] for j in range(PACK)]
         value_scales = keep.tile([P, PACK * P], U8, name="value_scales", align_bytes=64)
-        early_ps = [psum2.tile([P, 2, P], F32, name="turn_ps", tag="turn_ps") for b in range(Q_BLOCKS)]
-        late_ps = [psum.tile([P, 2, P], F32, name=f"late_ps{b}") for b in range(Q_BLOCKS)]
+        late_ps = [bank(6 + b, [P, 2, P], f"late_ps{b}") for b in range(Q_BLOCKS)]
         result = keep.tile([P, PACK, Q], F32, name="result")
         result_bf = keep.tile([P, Q, PACK], BF16, name="result_bf", align_bytes=64)
         out_planes = out_0.rearrange("(p j) q -> p j q", j=PACK)
 
-        def quantise_values(tile, planes):
+        def quantise_values(j):
             nc.vector.quantize_mx(
-                out=codes[:, Q + planes.start * P : Q + planes.stop * P].bitcast(FP8X4),
-                scales=value_scales[:, planes.start * P : planes.stop * P],
-                in_=tile[:].rearrange("s j m t -> s (j m t)"),
+                out=value_codes[j].bitcast(FP8X4),
+                scales=value_scales[:, j * P : (j + 1) * P],
+                in_=value_bf[j][:].rearrange("s m t -> s (m t)"),
             )
 
-        def multiply(j, cols, bank):
+        def multiply(j, cols, target):
             nc.tensor.matmul_mx(
-                out=bank,
-                lhsT=codes[:, Q + j * P : Q + (j + 1) * P].bitcast(FP8X4),
+                out=target,
+                lhsT=value_codes[j].bitcast(FP8X4),
                 lhsT_scale=value_scales[:, j * P : (j + 1) * P],
                 rhs=weight_codes[:, cols].bitcast(FP8X4),
                 rhs_scale=weight_scales[:, cols],
@@ -249,22 +255,23 @@ def tile_attend_valueresidual_pl_kernel(
                 stop=True,
             )
 
-        for tile, (planes, tag) in zip(group_bf[:-1], groups[:-1]):
-            quantise_values(tile, planes)
-        nc.vector.tensor_copy(value_bf[last][:, :, 0:2], halves[0][:].rearrange("s t m -> s m t"))
+        quantise_values(0)
+        quantise_values(1)
+        round_values(2)
+        round_values(last)
+        quantise_values(2)
         blocks = [slice(b * P, (b + 1) * P) for b in range(Q_BLOCKS)]
-        for b in range(Q_BLOCKS):
-            for j in range(2):
-                multiply(j, blocks[b], early_ps[b][:, j, :])
+        early_ps = bank(4, [P, 2, Q], "early_ps")
+        for j in range(2):
+            multiply(j, slice(0, Q), early_ps[:, j, :])
         for b in range(Q_BLOCKS):
             multiply(2, blocks[b], late_ps[b][:, 0, :])
-        plane_2_ps = psum.tile([P, Q], F32, name="plane_2_ps", tag="mixed_ps")
+        plane_2_ps = bank(2, [P, Q], "plane_2_ps")
         multiply(2, slice(0, Q), plane_2_ps[:])
-        quantise_values(group_bf[-1], groups[-1][0])
+        quantise_values(last)
         for b in range(Q_BLOCKS):
             multiply(last, blocks[b], late_ps[b][:, 1, :])
-        for b in range(Q_BLOCKS):
-            nc.scalar.copy(result[:, 0:2, blocks[b]], early_ps[b][:])
+        nc.scalar.copy(result[:, 0:2, :], early_ps[:])
         nc.vector.tensor_copy(result_bf[:, 0:P, 0:2], result[:, 0:2, 0:P].rearrange("p j q -> p q j"))
         nc.gpsimd.tensor_scalar(
             result_bf[:, P:Q, 0:2], result[:, 0:2, P:Q].rearrange("p j q -> p q j"), 1.0, 0.0, ALU.mult, ALU.add

@@ -34,6 +34,7 @@ def tile_attend_valueresidual_pl_kernel(
     nc = tc.nc
     with ExitStack() as ctx:
         keep = ctx.enter_context(tc.tile_pool(name="keep", bufs=1))
+        shared = ctx.enter_context(tc.tile_pool(name="shared", bufs=1))
         psum = ctx.enter_context(tc.psum_pool(name="psum", bufs=1))
 
         def bank(k, shape, name):
@@ -60,7 +61,10 @@ def tile_attend_valueresidual_pl_kernel(
         pool_sb = {}
 
         def load(j, pool):
-            pool_sb[j, pool] = keep.tile([P, T], F32, name=f"pool{j}_{pool}", align_bytes=64)
+            if (j, pool) == (PACK - 1, FIRST):
+                pool_sb[j, pool] = shared.tile([P, T], F32, name="last_window", offset=0, align_bytes=64)
+            else:
+                pool_sb[j, pool] = keep.tile([P, T], F32, name=f"pool{j}_{pool}", align_bytes=64)
             nc.sync.dma_start(pool_sb[j, pool][:], planes_hbm[pool][:, j, :])
 
         load(0, VALS)
@@ -179,7 +183,13 @@ def tile_attend_valueresidual_pl_kernel(
                     cols = slice(half * I // 2, (half + 1) * I // 2)
                     listed = pool_sb[j, pool][:].indirect(offsets[:, cols.start // 16 : cols.stop // 16])
                     nc.scalar.activation(plain[:, cols], listed, ACT.Copy)
-                    nc.gpsimd.tensor_tensor(picked[:, cols], plain[:, cols], ratio_row[:, cols], ALU.mult)
+                    words = slice(cols.start // PACK, cols.stop // PACK)
+                    nc.gpsimd.tensor_tensor(
+                        picked[:].rearrange("e (t s) -> e s t", t=PACK)[:, words, :],
+                        plain[:, cols].rearrange("e (s t) -> e s t", t=PACK),
+                        ratio_row[:, cols].rearrange("e (s t) -> e s t", t=PACK),
+                        ALU.mult,
+                    )
             else:
                 nc.vector.tensor_tensor(picked[:], listed, ratio_row[:], ALU.mult)
             return picked
@@ -191,15 +201,18 @@ def tile_attend_valueresidual_pl_kernel(
         for j in range(PACK):
             mixed = bank(mixed_banks[j], [P, PACK, P], f"mixed{j}")
             all_mixed.append(mixed)
-            for pool in (VALS, FIRST):
-                by_place = pick(j, pool)[:].rearrange("e (s t) -> e t s", t=PACK)
+            picks = {pool: pick(j, pool) for pool in (VALS, FIRST)}
+            pools = (FIRST, VALS) if j == 0 else (VALS, FIRST)
+            for pool in pools:
+                layout = "e (t s) -> e t s" if (j, pool) == (0, VALS) else "e (s t) -> e t s"
+                by_place = picks[pool][:].rearrange(layout, t=PACK)
                 for t in range(PACK):
                     nc.tensor.matmul(
                         mixed[:, t, :],
                         by_place[:, t, :],
                         ident[:],
-                        start=(pool == VALS and t == 0),
-                        stop=(pool == FIRST and t == PACK - 1),
+                        start=(pool == pools[0] and t == 0),
+                        stop=(pool == pools[1] and t == PACK - 1),
                         is_transpose=True,
                     )
             if j == 0:
@@ -209,7 +222,10 @@ def tile_attend_valueresidual_pl_kernel(
         value_bf = []
 
         def round_values(j):
-            tile = keep.tile([P, P, PACK], BF16, name=f"value_bf{j}", tag=value_tags[j], align_bytes=64)
+            if j == 2:
+                tile = shared.tile([P, P, PACK], BF16, name="value_bf2", offset=2 * T, align_bytes=64)
+            else:
+                tile = keep.tile([P, P, PACK], BF16, name=f"value_bf{j}", tag=value_tags[j], align_bytes=64)
             nc.vector.tensor_tensor(
                 tile[:],
                 all_mixed[j][:].rearrange("s t m -> s m t"),
@@ -228,7 +244,7 @@ def tile_attend_valueresidual_pl_kernel(
             in_=weights_bf[:].rearrange("p q t -> p (q t)"),
         )
 
-        early_codes = keep.tile([P, 2 * P], U32, name="early_codes", align_bytes=64)
+        early_codes = shared.tile([P, 2 * P], U32, name="early_codes", offset=0, align_bytes=64)
         late_codes = keep.tile([P, 2 * P], U32, name="late_codes", tag=f"picked{last}_{FIRST}", align_bytes=64)
         value_codes = [(early_codes, late_codes)[j // 2][:, j % 2 * P : (j % 2 + 1) * P] for j in range(PACK)]
         value_scales = keep.tile([P, PACK * P], U8, name="value_scales", align_bytes=64)
@@ -261,28 +277,22 @@ def tile_attend_valueresidual_pl_kernel(
         round_values(last)
         quantise_values(2)
         blocks = [slice(b * P, (b + 1) * P) for b in range(Q_BLOCKS)]
-        early_ps = bank(4, [P, 2, Q], "early_ps")
+        early_ps = bank(0, [P, 2, Q], "early_ps")
         for j in range(2):
             multiply(j, slice(0, Q), early_ps[:, j, :])
         for b in range(Q_BLOCKS):
             multiply(2, blocks[b], late_ps[b][:, 0, :])
-        plane_2_ps = bank(2, [P, Q], "plane_2_ps")
-        multiply(2, slice(0, Q), plane_2_ps[:])
         quantise_values(last)
         for b in range(Q_BLOCKS):
             multiply(last, blocks[b], late_ps[b][:, 1, :])
         nc.scalar.copy(result[:, 0:2, :], early_ps[:])
-        nc.vector.tensor_copy(result_bf[:, 0:P, 0:2], result[:, 0:2, 0:P].rearrange("p j q -> p q j"))
-        nc.gpsimd.tensor_scalar(
-            result_bf[:, P:Q, 0:2], result[:, 0:2, P:Q].rearrange("p j q -> p q j"), 1.0, 0.0, ALU.mult, ALU.add
-        )
+        nc.scalar.copy(result_bf[:, :, 0:2], early_ps[:].rearrange("p j q -> p q j"))
         nc.sync.dma_start(out_planes[:, 0:2, :], result[:, 0:2, :])
-        nc.scalar.copy(result[:, 2, :], plane_2_ps[:])
 
         nc.vector.tensor_copy(result_bf[:, 0:P, 2:PACK], late_ps[0][:].rearrange("p j q -> p q j"))
         nc.scalar.copy(result_bf[:, P:Q, 2:PACK], late_ps[1][:].rearrange("p j q -> p q j"))
-        nc.vector.tensor_copy(result[:, last, 0:P], late_ps[0][:, 1, :])
-        nc.scalar.copy(result[:, last, P:Q], late_ps[1][:, 1, :])
+        nc.vector.tensor_copy(result[:, 2:PACK, 0:P], late_ps[0][:])
+        nc.scalar.copy(result[:, 2:PACK, P:Q], late_ps[1][:])
         nc.scalar.dma_start(out_planes[:, 2:PACK, :], result[:, 2:PACK, :])
         result_codes = keep.tile([P, Q], U32, name="result_codes", align_bytes=64)
         result_scales = keep.tile([P, Q], U8, name="result_scales", align_bytes=64)

@@ -34,7 +34,6 @@ def tile_attend_valueresidual_pl_kernel(
     nc = tc.nc
     with ExitStack() as ctx:
         keep = ctx.enter_context(tc.tile_pool(name="keep", bufs=1))
-        shared = ctx.enter_context(tc.tile_pool(name="shared", bufs=1))
         psum = ctx.enter_context(tc.psum_pool(name="psum", bufs=1))
 
         def bank(k, shape, name):
@@ -61,10 +60,7 @@ def tile_attend_valueresidual_pl_kernel(
         pool_sb = {}
 
         def load(j, pool):
-            if (j, pool) == (PACK - 1, FIRST):
-                pool_sb[j, pool] = shared.tile([P, T], F32, name="last_window", offset=0, align_bytes=64)
-            else:
-                pool_sb[j, pool] = keep.tile([P, T], F32, name=f"pool{j}_{pool}", align_bytes=64)
+            pool_sb[j, pool] = keep.tile([P, T], F32, name=f"pool{j}_{pool}", align_bytes=64)
             nc.sync.dma_start(pool_sb[j, pool][:], planes_hbm[pool][:, j, :])
 
         load(0, VALS)
@@ -222,10 +218,7 @@ def tile_attend_valueresidual_pl_kernel(
         value_bf = []
 
         def round_values(j):
-            if j == 2:
-                tile = shared.tile([P, P, PACK], BF16, name="value_bf2", offset=2 * T, align_bytes=64)
-            else:
-                tile = keep.tile([P, P, PACK], BF16, name=f"value_bf{j}", tag=value_tags[j], align_bytes=64)
+            tile = keep.tile([P, P, PACK], BF16, name=f"value_bf{j}", tag=value_tags[j], align_bytes=64)
             nc.vector.tensor_tensor(
                 tile[:],
                 all_mixed[j][:].rearrange("s t m -> s m t"),
@@ -244,11 +237,11 @@ def tile_attend_valueresidual_pl_kernel(
             in_=weights_bf[:].rearrange("p q t -> p (q t)"),
         )
 
-        early_codes = shared.tile([P, 2 * P], U32, name="early_codes", offset=0, align_bytes=64)
+        early_codes = keep.tile([P, 2 * P], U32, name="early_codes", align_bytes=64)
         late_codes = keep.tile([P, 2 * P], U32, name="late_codes", tag=f"picked{last}_{FIRST}", align_bytes=64)
         value_codes = [(early_codes, late_codes)[j // 2][:, j % 2 * P : (j % 2 + 1) * P] for j in range(PACK)]
         value_scales = keep.tile([P, PACK * P], U8, name="value_scales", align_bytes=64)
-        late_ps = [bank(6 + b, [P, 2, P], f"late_ps{b}") for b in range(Q_BLOCKS)]
+        late_ps = [bank(b, [P, 2, P], f"late_ps{b}") for b in range(Q_BLOCKS)]
         result = keep.tile([P, PACK, Q], F32, name="result")
         result_bf = keep.tile([P, Q, PACK], BF16, name="result_bf", align_bytes=64)
         out_planes = out_0.rearrange("(p j) q -> p j q", j=PACK)
@@ -277,16 +270,19 @@ def tile_attend_valueresidual_pl_kernel(
         round_values(last)
         quantise_values(2)
         blocks = [slice(b * P, (b + 1) * P) for b in range(Q_BLOCKS)]
-        early_ps = bank(0, [P, 2, Q], "early_ps")
-        for j in range(2):
-            multiply(j, slice(0, Q), early_ps[:, j, :])
+        early_ps = bank(4, [P, Q_BLOCKS, PACK, P], "early_ps")
+        for b in range(Q_BLOCKS):
+            for j in range(2):
+                multiply(j, blocks[b], early_ps[:, b, j, :])
         for b in range(Q_BLOCKS):
             multiply(2, blocks[b], late_ps[b][:, 0, :])
         quantise_values(last)
         for b in range(Q_BLOCKS):
             multiply(last, blocks[b], late_ps[b][:, 1, :])
-        nc.scalar.copy(result[:, 0:2, :], early_ps[:])
-        nc.scalar.copy(result_bf[:, :, 0:2], early_ps[:].rearrange("p j q -> p q j"))
+        for b in range(Q_BLOCKS):
+            nc.scalar.copy(result[:, 0:2, blocks[b]], early_ps[:, b, 0:2, :])
+        nc.vector.tensor_copy(result_bf[:, 0:P, 0:2], result[:, 0:2, 0:P].rearrange("p j q -> p q j"))
+        nc.scalar.copy(result_bf[:, P:Q, 0:2], early_ps[:, 1, 0:2, :].rearrange("p j q -> p q j"))
         nc.sync.dma_start(out_planes[:, 0:2, :], result[:, 0:2, :])
 
         nc.vector.tensor_copy(result_bf[:, 0:P, 2:PACK], late_ps[0][:].rearrange("p j q -> p q j"))

@@ -34,6 +34,7 @@ def tile_attend_valueresidual_pl_kernel(
     nc = tc.nc
     with ExitStack() as ctx:
         keep = ctx.enter_context(tc.tile_pool(name="keep", bufs=1))
+        shared = ctx.enter_context(tc.tile_pool(name="shared", bufs=1))
         psum = ctx.enter_context(tc.psum_pool(name="psum", bufs=1))
 
         def bank(k, shape, name):
@@ -60,7 +61,7 @@ def tile_attend_valueresidual_pl_kernel(
         pool_sb = {}
 
         def load(j, pool):
-            pool_sb[j, pool] = keep.tile([P, T], F32, name=f"pool{j}_{pool}", align_bytes=64)
+            pool_sb[j, pool] = keep.tile([P, T], F32, name=f"pool{j}_{pool}", tag=f"pool{j}_{pool}", align_bytes=64)
             nc.sync.dma_start(pool_sb[j, pool][:], planes_hbm[pool][:, j, :])
 
         load(0, VALS)
@@ -70,7 +71,7 @@ def tile_attend_valueresidual_pl_kernel(
         nc.sync.dma_start(vsc_col[:], vsc.rearrange("(p t) o -> p (t o)", t=PACK))
         size_col = keep.tile([P, PACK], F32, name="size_col", align_bytes=64)
         nc.sync.dma_start(size_col[:], size.rearrange("o (p t) -> (o p) t", t=PACK))
-        for j, pool in ((2, VALS), (1, FIRST), (3, VALS), (2, FIRST), (3, FIRST)):
+        for j, pool in ((1, FIRST), (2, VALS), (3, VALS), (2, FIRST), (3, FIRST)):
             load(j, pool)
 
         ident = keep.tile([P, P], F32, name="ident")
@@ -119,7 +120,7 @@ def tile_attend_valueresidual_pl_kernel(
             ALU.add,
         )
 
-        row_sums = keep.tile([P, Q_BLOCKS], F32, name="row_sums", align_bytes=64)
+        row_sums = [keep.tile([P, 1], F32, name=f"row_sum{b}", align_bytes=64) for b in range(Q_BLOCKS)]
         all_probs = []
         for b in range(Q_BLOCKS):
             cols = slice(b * P, (b + 1) * P)
@@ -135,41 +136,28 @@ def tile_attend_valueresidual_pl_kernel(
             )
             neg_max = keep.tile([P, 1], F32, name=f"neg_max{b}", align_bytes=64)
             nc.vector.tensor_reduce(neg_max[:], scores[:], AXIS_X, ALU.max, negate=True)
-            probs = keep.tile([P, PACK, P], F32, name=f"probs{b}", align_bytes=64)
+            if b == 0:
+                probs = shared.tile([P, PACK, P], F32, name="probs0", offset=0, align_bytes=64)
+            else:
+                probs = keep.tile([P, PACK, P], F32, name="probs1", align_bytes=64)
             nc.scalar.activation(
                 probs[:],
                 scores[:].rearrange("q (s t) -> q t s", t=PACK),
                 ACT.Exp,
                 bias=neg_max[:],
-                accum_out=row_sums[:, b : b + 1],
+                accum_out=row_sums[b][:],
             )
             all_probs.append(probs)
-        inv_sums = keep.tile([P, Q_BLOCKS], F32, name="inv_sums")
-        nc.vector.reciprocal(inv_sums[:], row_sums[:])
-        weights_bf = keep.tile([P, Q, PACK], BF16, name="weights_bf", align_bytes=64)
-        for b in range(Q_BLOCKS):
-            norm = keep.tile([P, PACK, P], F32, name=f"norm{b}", align_bytes=64)
-            nc.scalar.activation(norm[:], all_probs[b][:], ACT.Copy, scale=inv_sums[:, b : b + 1])
-            turned = bank(b, [P, PACK, P], f"turned{b}")
-            for t in range(PACK):
-                nc.tensor.transpose(turned[:, t, :], norm[:, t, :], ident[:])
-            nc.vector.tensor_tensor(
-                weights_bf[:, b * P : (b + 1) * P, :],
-                turned[:].rearrange("s t q -> s q t"),
-                size_col[:].unsqueeze(1).to_broadcast([P, P, PACK]),
-                ALU.mult,
-            )
-
         picked_tags = {
             (1, VALS): "key_words_g",
-            (2, VALS): "neg_max1",
-            (3, VALS): "norm1",
-            (1, FIRST): "row_sums",
         }
 
         def pick(j, pool):
             tag = picked_tags.get((j, pool), f"picked{j}_{pool}")
-            picked = keep.tile([P, I], F32, name=f"picked{j}_{pool}", tag=tag, align_bytes=64)
+            if (j, pool) == (2, VALS):
+                picked = shared.tile([P, I], F32, name="picked2_vals", offset=0, align_bytes=64)
+            else:
+                picked = keep.tile([P, I], F32, name=f"picked{j}_{pool}", tag=tag, align_bytes=64)
             listed = pool_sb[j, pool][:].indirect(offsets[:])
             if pool == FIRST:
                 nc.scalar.activation(picked[:], listed, ACT.Copy)
@@ -179,29 +167,37 @@ def tile_attend_valueresidual_pl_kernel(
                     cols = slice(half * I // 2, (half + 1) * I // 2)
                     listed = pool_sb[j, pool][:].indirect(offsets[:, cols.start // 16 : cols.stop // 16])
                     nc.scalar.activation(plain[:, cols], listed, ACT.Copy)
-                    words = slice(cols.start // PACK, cols.stop // PACK)
-                    nc.gpsimd.tensor_tensor(
-                        picked[:].rearrange("e (t s) -> e s t", t=PACK)[:, words, :],
-                        plain[:, cols].rearrange("e (s t) -> e s t", t=PACK),
-                        ratio_row[:, cols].rearrange("e (s t) -> e s t", t=PACK),
-                        ALU.mult,
-                    )
+                    nc.gpsimd.tensor_tensor(picked[:, cols], plain[:, cols], ratio_row[:, cols], ALU.mult)
             else:
                 nc.vector.tensor_tensor(picked[:], listed, ratio_row[:], ALU.mult)
             return picked
 
+        vals_1 = pick(1, VALS)
+        all_turned = []
+        for b in range(Q_BLOCKS):
+            norm = keep.tile([P, PACK, P], F32, name=f"norm{b}", align_bytes=64)
+            inv_sum = keep.tile([P, 1], F32, name=f"inv_sum{b}")
+            nc.vector.reciprocal(inv_sum[:], row_sums[b][:])
+            if b == 0:
+                nc.gpsimd.tensor_scalar(norm[:], all_probs[b][:], inv_sum[:], 0.0, ALU.mult, ALU.add)
+            else:
+                nc.scalar.activation(norm[:], all_probs[b][:], ACT.Copy, scale=inv_sum[:])
+            turned = bank(b, [P, PACK, P], f"turned{b}")
+            for t in range(PACK):
+                nc.tensor.transpose(turned[:, t, :], norm[:, t, :], ident[:])
+            all_turned.append(turned)
+
         last = PACK - 1
-        value_tags = ("probs0", "value_bf1", "value_bf2", f"value_bf{last}")
+        value_tags = ("row_sum0", "value_bf1", "value_bf2", f"value_bf{last}")
         mixed_banks = (2, 3, 4, 5)
         all_mixed = []
         for j in range(PACK):
             mixed = bank(mixed_banks[j], [P, PACK, P], f"mixed{j}")
             all_mixed.append(mixed)
-            picks = {pool: pick(j, pool) for pool in (VALS, FIRST)}
+            picks = {pool: vals_1 if (j, pool) == (1, VALS) else pick(j, pool) for pool in (VALS, FIRST)}
             pools = (FIRST, VALS) if j == 0 else (VALS, FIRST)
             for pool in pools:
-                layout = "e (t s) -> e t s" if (j, pool) == (0, VALS) else "e (s t) -> e t s"
-                by_place = picks[pool][:].rearrange(layout, t=PACK)
+                by_place = picks[pool][:].rearrange("e (s t) -> e t s", t=PACK)
                 for t in range(PACK):
                     nc.tensor.matmul(
                         mixed[:, t, :],
@@ -216,11 +212,15 @@ def tile_attend_valueresidual_pl_kernel(
                 nc.gpsimd.tensor_tensor(outer[:], share[:], vsc_col[:], ALU.mult)
 
         value_bf = []
+        joint_bf = shared.tile([P, Q + P, PACK], BF16, name="joint_bf", offset=0, align_bytes=64)
 
         def round_values(j):
-            tile = keep.tile([P, P, PACK], BF16, name=f"value_bf{j}", tag=value_tags[j], align_bytes=64)
+            if j == 1:
+                tile = joint_bf[:, Q : Q + P, :]
+            else:
+                tile = keep.tile([P, P, PACK], BF16, name=f"value_bf{j}", tag=value_tags[j], align_bytes=64)[:]
             nc.vector.tensor_tensor(
-                tile[:],
+                tile,
                 all_mixed[j][:].rearrange("s t m -> s m t"),
                 outer[:].unsqueeze(1).to_broadcast([P, P, PACK]),
                 ALU.mult,
@@ -229,35 +229,41 @@ def tile_attend_valueresidual_pl_kernel(
 
         round_values(0)
         round_values(1)
-        weight_codes = keep.tile([P, Q], U32, name="weight_codes", align_bytes=64)
-        weight_scales = keep.tile([P, Q], U8, name="weight_scales", align_bytes=64)
-        nc.vector.quantize_mx(
-            out=weight_codes[:].bitcast(FP8X4),
-            scales=weight_scales[:],
-            in_=weights_bf[:].rearrange("p q t -> p (q t)"),
-        )
-
-        early_codes = keep.tile([P, 2 * P], U32, name="early_codes", align_bytes=64)
+        for b, turned in enumerate(all_turned):
+            nc.vector.tensor_tensor(
+                joint_bf[:, b * P : (b + 1) * P, :],
+                turned[:].rearrange("s t q -> s q t"),
+                size_col[:].unsqueeze(1).to_broadcast([P, P, PACK]),
+                ALU.mult,
+            )
+        round_values(2)
+        early_codes = keep.tile([P, Q + 2 * P], U32, name="early_codes", tag=f"pool{last}_{FIRST}", align_bytes=64)
         late_codes = keep.tile([P, 2 * P], U32, name="late_codes", tag=f"picked{last}_{FIRST}", align_bytes=64)
-        value_codes = [(early_codes, late_codes)[j // 2][:, j % 2 * P : (j % 2 + 1) * P] for j in range(PACK)]
-        value_scales = keep.tile([P, PACK * P], U8, name="value_scales", align_bytes=64)
+        scales = keep.tile([P, Q + PACK * P], U8, name="scales", align_bytes=64)
+        nc.vector.quantize_mx(
+            out=early_codes[:, 0 : Q + P].bitcast(FP8X4),
+            scales=scales[:, 0 : Q + P],
+            in_=joint_bf[:].rearrange("p q t -> p (q t)"),
+        )
+        weight_codes, weight_scales = early_codes[:, 0:Q], scales[:, 0:Q]
+        value_codes = [early_codes[:, Q + P :], early_codes[:, Q : Q + P], late_codes[:, 0:P], late_codes[:, P:]]
+        value_scales = [scales[:, Q + k * P : Q + (k + 1) * P] for k in (1, 0, 2, 3)]
         late_ps = [bank(b, [P, 2, P], f"late_ps{b}") for b in range(Q_BLOCKS)]
         result = keep.tile([P, PACK, Q], F32, name="result")
-        result_bf = keep.tile([P, Q, PACK], BF16, name="result_bf", align_bytes=64)
         out_planes = out_0.rearrange("(p j) q -> p j q", j=PACK)
 
         def quantise_values(j):
             nc.vector.quantize_mx(
                 out=value_codes[j].bitcast(FP8X4),
-                scales=value_scales[:, j * P : (j + 1) * P],
-                in_=value_bf[j][:].rearrange("s m t -> s (m t)"),
+                scales=value_scales[j],
+                in_=value_bf[j].rearrange("s m t -> s (m t)"),
             )
 
         def multiply(j, cols, target):
             nc.tensor.matmul_mx(
                 out=target,
                 lhsT=value_codes[j].bitcast(FP8X4),
-                lhsT_scale=value_scales[:, j * P : (j + 1) * P],
+                lhsT_scale=value_scales[j],
                 rhs=weight_codes[:, cols].bitcast(FP8X4),
                 rhs_scale=weight_scales[:, cols],
                 start=True,
@@ -265,24 +271,23 @@ def tile_attend_valueresidual_pl_kernel(
             )
 
         quantise_values(0)
-        quantise_values(1)
-        round_values(2)
         round_values(last)
         quantise_values(2)
         blocks = [slice(b * P, (b + 1) * P) for b in range(Q_BLOCKS)]
-        early_ps = bank(4, [P, Q_BLOCKS, PACK, P], "early_ps")
+        early_ps = [bank(6 + b, [P, 2, P], f"early_ps{b}") for b in range(Q_BLOCKS)]
         for b in range(Q_BLOCKS):
-            for j in range(2):
-                multiply(j, blocks[b], early_ps[:, b, j, :])
+            for j in (1, 0):
+                multiply(j, blocks[b], early_ps[b][:, j, :])
         for b in range(Q_BLOCKS):
             multiply(2, blocks[b], late_ps[b][:, 0, :])
         quantise_values(last)
         for b in range(Q_BLOCKS):
             multiply(last, blocks[b], late_ps[b][:, 1, :])
+        result_bf = keep.tile([P, Q, PACK], BF16, name="result_bf", tag=f"value_bf{last}", align_bytes=64)
         for b in range(Q_BLOCKS):
-            nc.scalar.copy(result[:, 0:2, blocks[b]], early_ps[:, b, 0:2, :])
+            nc.scalar.copy(result[:, 0:2, blocks[b]], early_ps[b][:])
         nc.vector.tensor_copy(result_bf[:, 0:P, 0:2], result[:, 0:2, 0:P].rearrange("p j q -> p q j"))
-        nc.scalar.copy(result_bf[:, P:Q, 0:2], early_ps[:, 1, 0:2, :].rearrange("p j q -> p q j"))
+        nc.scalar.copy(result_bf[:, P:Q, 0:2], early_ps[1][:].rearrange("p j q -> p q j"))
         nc.sync.dma_start(out_planes[:, 0:2, :], result[:, 0:2, :])
 
         nc.vector.tensor_copy(result_bf[:, 0:P, 2:PACK], late_ps[0][:].rearrange("p j q -> p q j"))

@@ -69,10 +69,11 @@ def tile_attend_valueresidual_pl_kernel(
         load(1, VALS)
         vsc_col = keep.tile([P, PACK], F32, name="vsc_col")
         nc.sync.dma_start(vsc_col[:], vsc.rearrange("(p t) o -> p (t o)", t=PACK))
+        for j, pool in ((1, FIRST), (2, VALS), (3, VALS), (2, FIRST)):
+            load(j, pool)
         size_col = keep.tile([P, PACK], F32, name="size_col", align_bytes=64)
         nc.sync.dma_start(size_col[:], size.rearrange("o (p t) -> (o p) t", t=PACK))
-        for j, pool in ((1, FIRST), (2, VALS), (3, VALS), (2, FIRST), (3, FIRST)):
-            load(j, pool)
+        load(3, FIRST)
 
         ident = keep.tile([P, P], F32, name="ident")
         make_identity(nc, ident[:])

@@ -24,6 +24,9 @@ Q_BLOCKS = Q // P
 QUADRANTS = 4
 SCALE_ROWS = 4
 WALK = 4
+SCALAR_SLOTS = 256
+SCALAR_ROWS = 48
+VECTOR_SLOTS = 128
 VALS, FIRST = 0, 1
 TINY = 2.0**-60
 
@@ -69,11 +72,12 @@ def tile_attend_valueresidual_pl_kernel(
         load(1, VALS)
         vsc_col = keep.tile([P, PACK], F32, name="vsc_col")
         nc.sync.dma_start(vsc_col[:], vsc.rearrange("(p t) o -> p (t o)", t=PACK))
-        for j, pool in ((1, FIRST), (2, VALS), (3, VALS), (2, FIRST)):
-            load(j, pool)
+        load(1, FIRST)
+        load(2, VALS)
         size_col = keep.tile([P, PACK], F32, name="size_col", align_bytes=64)
         nc.sync.dma_start(size_col[:], size.rearrange("o (p t) -> (o p) t", t=PACK))
-        load(3, FIRST)
+        for j, pool in ((3, VALS), (2, FIRST), (3, FIRST)):
+            load(j, pool)
 
         ident = keep.tile([P, P], F32, name="ident")
         make_identity(nc, ident[:])
@@ -160,7 +164,11 @@ def tile_attend_valueresidual_pl_kernel(
             else:
                 picked = keep.tile([P, I], F32, name=f"picked{j}_{pool}", tag=tag, align_bytes=64)
             listed = pool_sb[j, pool][:].indirect(offsets[:])
-            if pool == FIRST:
+            if (j, pool) == (PACK - 1, FIRST):
+                cut = I - VECTOR_SLOTS
+                nc.scalar.activation(picked[:, 0:cut], pool_sb[j, pool][:].indirect(offsets[:, 0 : cut // 16]), ACT.Copy)
+                nc.vector.tensor_copy(picked[:, cut:], pool_sb[j, pool][:].indirect(offsets[:, cut // 16 :]))
+            elif pool == FIRST:
                 nc.scalar.activation(picked[:], listed, ACT.Copy)
             elif j == 0:
                 plain = keep.tile([P, I], F32, name="plain")
@@ -169,6 +177,13 @@ def tile_attend_valueresidual_pl_kernel(
                     listed = pool_sb[j, pool][:].indirect(offsets[:, cols.start // 16 : cols.stop // 16])
                     nc.scalar.activation(plain[:, cols], listed, ACT.Copy)
                     nc.gpsimd.tensor_tensor(picked[:, cols], plain[:, cols], ratio_row[:, cols], ALU.mult)
+            elif j == PACK - 1:
+                cut = slice(I - SCALAR_SLOTS, I)
+                listed = pool_sb[j, pool][:].indirect(offsets[:, 0 : cut.start // 16])
+                nc.vector.tensor_tensor(picked[:, 0 : cut.start], listed, ratio_row[:, 0 : cut.start], ALU.mult)
+                rest = keep.tile([P, SCALAR_SLOTS], F32, name="rest")
+                nc.scalar.activation(rest[:], pool_sb[j, pool][:].indirect(offsets[:, cut.start // 16 :]), ACT.Copy)
+                nc.gpsimd.tensor_tensor(picked[:, cut], rest[:], ratio_row[:, cut], ALU.mult)
             else:
                 nc.vector.tensor_tensor(picked[:], listed, ratio_row[:], ALU.mult)
             return picked
@@ -213,7 +228,7 @@ def tile_attend_valueresidual_pl_kernel(
                 nc.gpsimd.tensor_tensor(outer[:], share[:], vsc_col[:], ALU.mult)
 
         value_bf = []
-        joint_bf = shared.tile([P, Q + P, PACK], BF16, name="joint_bf", offset=0, align_bytes=64)
+        joint_bf = keep.tile([P, Q + P, PACK], BF16, name="joint_bf", tag=f"pool{last}_{VALS}", align_bytes=64)
 
         def round_values(j):
             if j == 1:
@@ -237,8 +252,19 @@ def tile_attend_valueresidual_pl_kernel(
                 size_col[:].unsqueeze(1).to_broadcast([P, P, PACK]),
                 ALU.mult,
             )
-        round_values(2)
-        early_codes = keep.tile([P, Q + 2 * P], U32, name="early_codes", tag=f"pool{last}_{FIRST}", align_bytes=64)
+        third_bf = keep.tile([P, P, PACK], BF16, name="third_bf", align_bytes=64)
+        nc.vector.tensor_tensor(
+            third_bf[:, SCALAR_ROWS:, :],
+            all_mixed[2][:, :, SCALAR_ROWS:].rearrange("s t m -> s m t"),
+            outer[:].unsqueeze(1).to_broadcast([P, P - SCALAR_ROWS, PACK]),
+            ALU.mult,
+        )
+        for t in range(PACK):
+            nc.scalar.activation(
+                third_bf[:, 0:SCALAR_ROWS, t], all_mixed[2][:, t, 0:SCALAR_ROWS], ACT.Copy, scale=outer[:, t : t + 1]
+            )
+        value_bf.append(third_bf[:])
+        early_codes = keep.tile([P, Q + 2 * P], U32, name="early_codes", tag=f"picked2_{FIRST}", align_bytes=64)
         late_codes = keep.tile([P, 2 * P], U32, name="late_codes", tag=f"picked{last}_{FIRST}", align_bytes=64)
         scales = keep.tile([P, Q + PACK * P], U8, name="scales", align_bytes=64)
         nc.vector.quantize_mx(

from contextlib import ExitStack

import concourse.mybir as mybir
from concourse.masks import make_identity

D, T, I, Q, E = 512, 1024, 512, 256, 512
FLOPS = 2 * Q * I * D + 2 * E * I * Q

F32 = mybir.dt.float32
BF16 = mybir.dt.bfloat16
I32 = mybir.dt.int32
U32 = mybir.dt.uint32
U16 = mybir.dt.uint16
U8 = mybir.dt.uint8
FP8X4 = mybir.dt.float8_e4m3fn_x4
FP4X4 = mybir.dt.float4_e2m1fn_x4
ALU = mybir.AluOpType
ACT = mybir.ActivationFunctionType
AXIS_X = mybir.AxisListType.X

P = 128
PACK = 4
Q_BLOCKS = Q // P
QUADRANTS = 4
SCALE_ROWS = 4
WALK = 4
SCALAR_SLOTS = 256
SCALAR_ROWS = 48
VECTOR_SLOTS = 128
VALS, FIRST = 0, 1
TINY = 2.0**-60


def tile_attend_valueresidual_pl_kernel(
    tc, query, keys_words, keys_scales, size, vals, first, lam, vsc, offs, out_0, out_1, out_2
):
    nc = tc.nc
    with ExitStack() as ctx:
        keep = ctx.enter_context(tc.tile_pool(name="keep", bufs=1))
        shared = ctx.enter_context(tc.tile_pool(name="shared", bufs=1))
        psum = ctx.enter_context(tc.psum_pool(name="psum", bufs=1))

        def bank(k, shape, name):
            return psum.tile(shape, F32, name=name, tag=f"bank{k}")

        offsets = keep.tile([P, I // 16], U16, name="offsets")
        nc.sync.dma_start(offsets[:], offs)

        key_scales = keep.tile([P, T], U8, name="key_scales", align_bytes=64)
        nc.gpsimd.memset(key_scales[:].bitcast(I32), 0)

        lam_col = keep.tile([P, PACK], F32, name="lam_col")
        nc.sync.dma_start(lam_col[:], lam.rearrange("o (p t) -> (o p) t", t=PACK))
        key_words = keep.tile([P, T], U16, name="key_words", align_bytes=64)
        nc.sync.dma_start(key_words[:].bitcast(I32), keys_words[0].bitcast(I32))
        for quad in range(QUADRANTS):
            nc.sync.dma_start(
                key_scales[32 * quad : 32 * quad + SCALE_ROWS, :].bitcast(I32),
                keys_scales[0, SCALE_ROWS * quad : SCALE_ROWS * (quad + 1), :].bitcast(I32),
            )
        query_sb = keep.tile([P, PACK, Q], F32, name="query_sb", tag="query_sb", align_bytes=64)
        nc.sync.dma_start(query_sb[:], query.rearrange("(p j) q -> p j q", j=PACK))
        planes_hbm = (vals.rearrange("(p j) n -> p j n", j=PACK), first.rearrange("(p j) n -> p j n", j=PACK))
        pool_sb = {}

        def load(j, pool):
            pool_sb[j, pool] = keep.tile([P, T], F32, name=f"pool{j}_{pool}", tag=f"pool{j}_{pool}", align_bytes=64)
            nc.sync.dma_start(pool_sb[j, pool][:], planes_hbm[pool][:, j, :])

        load(0, VALS)
        load(0, FIRST)
        load(1, VALS)
        vsc_col = keep.tile([P, PACK], F32, name="vsc_col")
        nc.sync.dma_start(vsc_col[:], vsc.rearrange("(p t) o -> p (t o)", t=PACK))
        load(1, FIRST)
        load(2, VALS)
        size_col = keep.tile([P, PACK], F32, name="size_col", align_bytes=64)
        nc.sync.dma_start(size_col[:], size.rearrange("o (p t) -> (o p) t", t=PACK))
        for j, pool in ((3, VALS), (2, FIRST), (3, FIRST)):
            load(j, pool)

        ident = keep.tile([P, P], F32, name="ident")
        make_identity(nc, ident[:])

        neg_share = keep.tile([P, PACK], F32, name="neg_share")
        nc.vector.tensor_scalar(neg_share[:], lam_col[:], 1.0, TINY, ALU.subtract, ALU.subtract)
        neg_inverse = keep.tile([P, PACK], F32, name="neg_inverse")
        nc.vector.reciprocal(neg_inverse[:], neg_share[:])
        neg_ratio = keep.tile([P, PACK], F32, name="neg_ratio")
        nc.gpsimd.tensor_tensor(neg_ratio[:], lam_col[:], neg_inverse[:], ALU.mult)
        share = keep.tile([P, PACK], F32, name="share")
        nc.gpsimd.tensor_scalar(share[:], neg_share[:], -1.0, 0.0, ALU.mult, ALU.add)

        spread = bank(2, [P, PACK, P], "spread")
        for t in range(PACK):
            nc.tensor.transpose(spread[:, t, :], neg_ratio[:, t : t + 1].to_broadcast([P, P]), ident[:])

        key_words_g = keep.tile([P, I], U16, name="key_words_g", align_bytes=64)
        nc.vector.tensor_copy(key_words_g[:], key_words[:].indirect(offsets[:]))
        key_scales_g = keep.tile([P, I], U8, name="key_scales_g", align_bytes=64)
        nc.vector.tensor_copy(key_scales_g[:], key_scales[:].indirect(offsets[:]))

        query_bf = keep.tile([P, Q, PACK], BF16, name="query_bf", align_bytes=64)
        query_codes = keep.tile([P, Q], U32, name="query_codes", align_bytes=64)
        query_scales = keep.tile([P, Q], U8, name="query_scales", align_bytes=64)
        for b in range(Q_BLOCKS):
            cols = slice(b * P, (b + 1) * P)
            nc.scalar.copy(
                query_bf[:, cols, :].rearrange("p (c i) t -> p c t i", i=WALK),
                query_sb[:, :, cols].rearrange("p t (c i) -> p c t i", i=WALK),
            )
            nc.vector.quantize_mx(
                out=query_codes[:, cols].bitcast(FP8X4),
                scales=query_scales[:, cols],
                in_=query_bf[:, cols, :].rearrange("p q t -> p (q t)"),
            )

        ratio_row = keep.tile([P, I], F32, name="ratio_row", tag="query_sb", align_bytes=64)
        nc.vector.tensor_scalar(
            ratio_row[:].rearrange("m (p t) -> m p t", t=PACK),
            spread[:].rearrange("m t p -> m p t"),
            -1.0,
            0.0,
            ALU.mult,
            ALU.add,
        )

        row_sums = [keep.tile([P, 1], F32, name=f"row_sum{b}", align_bytes=64) for b in range(Q_BLOCKS)]
        all_probs = []
        for b in range(Q_BLOCKS):
            cols = slice(b * P, (b + 1) * P)
            scores = bank(b, [P, I], f"scores{b}")
            nc.tensor.matmul_mx(
                out=scores[:],
                lhsT=query_codes[:, cols].bitcast(FP8X4),
                lhsT_scale=query_scales[:, cols],
                rhs=key_words_g[:].bitcast(FP4X4),
                rhs_scale=key_scales_g[:],
                start=True,
                stop=True,
            )
            neg_max = keep.tile([P, 1], F32, name=f"neg_max{b}", align_bytes=64)
            nc.vector.tensor_reduce(neg_max[:], scores[:], AXIS_X, ALU.max, negate=True)
            if b == 0:
                probs = shared.tile([P, PACK, P], F32, name="probs0", offset=0, align_bytes=64)
            else:
                probs = keep.tile([P, PACK, P], F32, name="probs1", align_bytes=64)
            nc.scalar.activation(
                probs[:],
                scores[:].rearrange("q (s t) -> q t s", t=PACK),
                ACT.Exp,
                bias=neg_max[:],
                accum_out=row_sums[b][:],
            )
            all_probs.append(probs)
        picked_tags = {
            (1, VALS): "key_words_g",
        }

        def pick(j, pool):
            tag = picked_tags.get((j, pool), f"picked{j}_{pool}")
            if (j, pool) == (2, VALS):
                picked = shared.tile([P, I], F32, name="picked2_vals", offset=0, align_bytes=64)
            else:
                picked = keep.tile([P, I], F32, name=f"picked{j}_{pool}", tag=tag, align_bytes=64)
            listed = pool_sb[j, pool][:].indirect(offsets[:])
            if (j, pool) == (PACK - 1, FIRST):
                cut = I - VECTOR_SLOTS
                nc.scalar.activation(picked[:, 0:cut], pool_sb[j, pool][:].indirect(offsets[:, 0 : cut // 16]), ACT.Copy)
                nc.vector.tensor_copy(picked[:, cut:], pool_sb[j, pool][:].indirect(offsets[:, cut // 16 :]))
            elif pool == FIRST:
                nc.scalar.activation(picked[:], listed, ACT.Copy)
            elif j == 0:
                plain = keep.tile([P, I], F32, name="plain")
                for half in range(2):
                    cols = slice(half * I // 2, (half + 1) * I // 2)
                    listed = pool_sb[j, pool][:].indirect(offsets[:, cols.start // 16 : cols.stop // 16])
                    nc.scalar.activation(plain[:, cols], listed, ACT.Copy)
                    nc.gpsimd.tensor_tensor(picked[:, cols], plain[:, cols], ratio_row[:, cols], ALU.mult)
            elif j == PACK - 1:
                cut = slice(I - SCALAR_SLOTS, I)
                listed = pool_sb[j, pool][:].indirect(offsets[:, 0 : cut.start // 16])
                nc.vector.tensor_tensor(picked[:, 0 : cut.start], listed, ratio_row[:, 0 : cut.start], ALU.mult)
                rest = keep.tile([P, SCALAR_SLOTS], F32, name="rest")
                nc.scalar.activation(rest[:], pool_sb[j, pool][:].indirect(offsets[:, cut.start // 16 :]), ACT.Copy)
                nc.gpsimd.tensor_tensor(picked[:, cut], rest[:], ratio_row[:, cut], ALU.mult)
            else:
                nc.vector.tensor_tensor(picked[:], listed, ratio_row[:], ALU.mult)
            return picked

        vals_1 = pick(1, VALS)
        all_turned = []
        for b in range(Q_BLOCKS):
            norm = keep.tile([P, PACK, P], F32, name=f"norm{b}", align_bytes=64)
            inv_sum = keep.tile([P, 1], F32, name=f"inv_sum{b}")
            nc.vector.reciprocal(inv_sum[:], row_sums[b][:])
            if b == 0:
                nc.gpsimd.tensor_scalar(norm[:], all_probs[b][:], inv_sum[:], 0.0, ALU.mult, ALU.add)
            else:
                nc.scalar.activation(norm[:], all_probs[b][:], ACT.Copy, scale=inv_sum[:])
            turned = bank(b, [P, PACK, P], f"turned{b}")
            for t in range(PACK):
                nc.tensor.transpose(turned[:, t, :], norm[:, t, :], ident[:])
            all_turned.append(turned)

        last = PACK - 1
        value_tags = ("row_sum0", "value_bf1", "value_bf2", f"value_bf{last}")
        mixed_banks = (2, 3, 4, 5)
        all_mixed = []
        for j in range(PACK):
            mixed = bank(mixed_banks[j], [P, PACK, P], f"mixed{j}")
            all_mixed.append(mixed)
            picks = {pool: vals_1 if (j, pool) == (1, VALS) else pick(j, pool) for pool in (VALS, FIRST)}
            pools = (FIRST, VALS) if j == 0 else (VALS, FIRST)
            for pool in pools:
                by_place = picks[pool][:].rearrange("e (s t) -> e t s", t=PACK)
                for t in range(PACK):
                    nc.tensor.matmul(
                        mixed[:, t, :],
                        by_place[:, t, :],
                        ident[:],
                        start=(pool == pools[0] and t == 0),
                        stop=(pool == pools[1] and t == PACK - 1),
                        is_transpose=True,
                    )
            if j == 0:
                outer = keep.tile([P, PACK], F32, name="outer", tag="plain")
                nc.gpsimd.tensor_tensor(outer[:], share[:], vsc_col[:], ALU.mult)

        value_bf = []
        joint_bf = keep.tile([P, Q + P, PACK], BF16, name="joint_bf", tag=f"pool{last}_{VALS}", align_bytes=64)

        def round_values(j):
            if j == 1:
                tile = joint_bf[:, Q : Q + P, :]
            else:
                tile = keep.tile([P, P, PACK], BF16, name=f"value_bf{j}", tag=value_tags[j], align_bytes=64)[:]
            nc.vector.tensor_tensor(
                tile,
                all_mixed[j][:].rearrange("s t m -> s m t"),
                outer[:].unsqueeze(1).to_broadcast([P, P, PACK]),
                ALU.mult,
            )
            value_bf.append(tile)

        round_values(0)
        round_values(1)
        for b, turned in enumerate(all_turned):
            nc.vector.tensor_tensor(
                joint_bf[:, b * P : (b + 1) * P, :],
                turned[:].rearrange("s t q -> s q t"),
                size_col[:].unsqueeze(1).to_broadcast([P, P, PACK]),
                ALU.mult,
            )
        third_bf = keep.tile([P, P, PACK], BF16, name="third_bf", align_bytes=64)
        nc.vector.tensor_tensor(
            third_bf[:, SCALAR_ROWS:, :],
            all_mixed[2][:, :, SCALAR_ROWS:].rearrange("s t m -> s m t"),
            outer[:].unsqueeze(1).to_broadcast([P, P - SCALAR_ROWS, PACK]),
            ALU.mult,
        )
        for t in range(PACK):
            nc.scalar.activation(
                third_bf[:, 0:SCALAR_ROWS, t], all_mixed[2][:, t, 0:SCALAR_ROWS], ACT.Copy, scale=outer[:, t : t + 1]
            )
        value_bf.append(third_bf[:])
        early_codes = keep.tile([P, Q + 2 * P], U32, name="early_codes", tag=f"picked2_{FIRST}", align_bytes=64)
        late_codes = keep.tile([P, 2 * P], U32, name="late_codes", tag=f"picked{last}_{FIRST}", align_bytes=64)
        scales = keep.tile([P, Q + PACK * P], U8, name="scales", align_bytes=64)
        nc.vector.quantize_mx(
            out=early_codes[:, 0 : Q + P].bitcast(FP8X4),
            scales=scales[:, 0 : Q + P],
            in_=joint_bf[:].rearrange("p q t -> p (q t)"),
        )
        weight_codes, weight_scales = early_codes[:, 0:Q], scales[:, 0:Q]
        value_codes = [early_codes[:, Q + P :], early_codes[:, Q : Q + P], late_codes[:, 0:P], late_codes[:, P:]]
        value_scales = [scales[:, Q + k * P : Q + (k + 1) * P] for k in (1, 0, 2, 3)]
        late_ps = [bank(b, [P, 2, P], f"late_ps{b}") for b in range(Q_BLOCKS)]
        result = keep.tile([P, PACK, Q], F32, name="result")
        out_planes = out_0.rearrange("(p j) q -> p j q", j=PACK)

        def quantise_values(j):
            nc.vector.quantize_mx(
                out=value_codes[j].bitcast(FP8X4),
                scales=value_scales[j],
                in_=value_bf[j].rearrange("s m t -> s (m t)"),
            )

        def multiply(j, cols, target):
            nc.tensor.matmul_mx(
                out=target,
                lhsT=value_codes[j].bitcast(FP8X4),
                lhsT_scale=value_scales[j],
                rhs=weight_codes[:, cols].bitcast(FP8X4),
                rhs_scale=weight_scales[:, cols],
                start=True,
                stop=True,
            )

        quantise_values(0)
        round_values(last)
        quantise_values(2)
        blocks = [slice(b * P, (b + 1) * P) for b in range(Q_BLOCKS)]
        early_ps = [bank(6 + b, [P, 2, P], f"early_ps{b}") for b in range(Q_BLOCKS)]
        for b in range(Q_BLOCKS):
            for j in (1, 0):
                multiply(j, blocks[b], early_ps[b][:, j, :])
        for b in range(Q_BLOCKS):
            multiply(2, blocks[b], late_ps[b][:, 0, :])
        quantise_values(last)
        for b in range(Q_BLOCKS):
            multiply(last, blocks[b], late_ps[b][:, 1, :])
        result_bf = keep.tile([P, Q, PACK], BF16, name="result_bf", tag=f"value_bf{last}", align_bytes=64)
        for b in range(Q_BLOCKS):
            nc.scalar.copy(result[:, 0:2, blocks[b]], early_ps[b][:])
        nc.vector.tensor_copy(result_bf[:, 0:P, 0:2], result[:, 0:2, 0:P].rearrange("p j q -> p q j"))
        nc.scalar.copy(result_bf[:, P:Q, 0:2], early_ps[1][:].rearrange("p j q -> p q j"))
        nc.sync.dma_start(out_planes[:, 0:2, :], result[:, 0:2, :])

        nc.vector.tensor_copy(result_bf[:, 0:P, 2:PACK], late_ps[0][:].rearrange("p j q -> p q j"))
        nc.scalar.copy(result_bf[:, P:Q, 2:PACK], late_ps[1][:].rearrange("p j q -> p q j"))
        nc.vector.tensor_copy(result[:, 2:PACK, 0:P], late_ps[0][:])
        nc.scalar.copy(result[:, 2:PACK, P:Q], late_ps[1][:])
        nc.scalar.dma_start(out_planes[:, 2:PACK, :], result[:, 2:PACK, :])
        result_codes = keep.tile([P, Q], U32, name="result_codes", align_bytes=64)
        result_scales = keep.tile([P, Q], U8, name="result_scales", align_bytes=64)
        nc.vector.quantize_mx(
            out=result_codes[:].bitcast(FP8X4),
            scales=result_scales[:],
            in_=result_bf[:].rearrange("p q j -> p (q j)"),
        )
        nc.sync.dma_start(
            out_1[0].rearrange("p q j -> p (q j)").bitcast(I32), result_codes[:].bitcast(I32)
        )
        for quad in range(QUADRANTS):
            queue = nc.scalar if quad % 2 == 0 else nc.sync
            queue.dma_start(
                out_2[0, SCALE_ROWS * quad : SCALE_ROWS * (quad + 1), :].bitcast(I32),
                result_scales[32 * quad : 32 * quad + SCALE_ROWS, :].bitcast(I32),
            )
